import numpy as np
import ml_dtypes


def mxq(x, axis, fmt="e4m3"):
    dtype, down = {"e4m3": (ml_dtypes.float8_e4m3fn, 7), "e5m2": (ml_dtypes.float8_e5m2, 14)}[fmt]
    v = np.moveaxis(np.asarray(x, np.float32).astype(ml_dtypes.bfloat16).astype(np.float64), axis, -1)
    blocks = v.reshape(v.shape[:-1] + (-1, 32))
    amax = np.abs(blocks).max(-1, keepdims=True)
    byte = np.maximum(np.where(amax > 0, np.frexp(amax)[1] - 1 + 127, 0) - down, 1)
    scale = np.exp2(byte - 127.0)
    codes = (blocks / scale).astype(np.float32).astype(dtype).astype(np.float64)
    return np.moveaxis((codes * scale).reshape(v.shape), -1, axis)


WIDE = False


def mx_kscale(k):
    if not WIDE:
        return np.ones(k)
    levels = np.array([10, -10, 5, -5, 0])
    if k % 512:
        return np.exp2(np.random.permutation(np.resize(levels, k // 32))).repeat(32)
    a = np.empty((k // 512, 16))
    for p in range(k // 512):
        a[p, :8] = np.random.permutation(np.resize(levels, 8))
        for g in range(8):
            far = levels[np.abs(levels - a[p, g]) >= 10]
            a[p, g + 8] = far[np.random.randint(len(far))]
    return np.exp2(a.ravel()).repeat(32)


def f64(x):
    return np.asarray(x).astype(np.float64)


def striped(idx):
    return np.tile(idx.reshape(-1, 16).T, (8, 1)).astype(np.uint16)


def unstriped(offs):
    return offs[:16].T.reshape(-1).astype(np.int64)


E2M1 = np.array([0.0, 0.5, 1.0, 1.5, 2.0, 3.0, 4.0, 6.0, -0.0, -0.5, -1.0, -1.5, -2.0, -3.0, -4.0, -6.0])


def pack_weight(w, fmt):
    k, n = w.shape
    w = f64(np.asarray(w, np.float32).astype(ml_dtypes.bfloat16)).reshape(k // 32, 32, n)
    amax = np.abs(w).max(1)
    if fmt == "e4m3":
        byte = np.frexp(amax)[1] - 1 + 127 - 7
    else:
        mant, ex = np.frexp(amax / 6.0)
        byte = np.where(mant > 0.5, ex, ex - 1) + 127
    byte = np.clip(np.where(amax > 0, byte, 1), 1, 254)
    scaled = (w * np.exp2(127.0 - byte)[:, None, :]).reshape(k, n).astype(np.float32)
    by_word = np.ascontiguousarray(scaled.reshape(k // 512, 128, 4, n).transpose(0, 1, 3, 2))
    if fmt == "e4m3":
        words = by_word.astype(ml_dtypes.float8_e4m3fn).view(np.uint8)
    else:
        c = by_word.astype(ml_dtypes.float4_e2m1fn).view(np.uint8) & 0xF
        words = (c[..., 0::2] | (c[..., 1::2] << 4)).reshape(k // 512, 128, 2 * n)
    return np.ascontiguousarray(words), np.ascontiguousarray(byte.astype(np.uint8).reshape(k // 512, 16, n))


def unpack_weight(words, scales, fmt):
    g, _, n = scales.shape
    words = np.ascontiguousarray(words).reshape(g, 128, n, -1)
    if fmt == "e4m3":
        vals = words.view(ml_dtypes.float8_e4m3fn).astype(np.float64)
    else:
        nib = np.empty((g, 128, n, 4), np.uint8)
        nib[..., 0::2] = words & 0xF
        nib[..., 1::2] = words >> 4
        vals = E2M1[nib]
    vals = vals * np.repeat(np.exp2(scales.astype(np.float64) - 127.0), 8, axis=1)[..., None]
    return vals.transpose(0, 1, 3, 2).reshape(g * 512, n)


def gelu(v):
    return 0.5 * v * (1.0 + np.tanh(np.sqrt(2.0 / np.pi) * (v + 0.044715 * v**3)))


def often(T, S):
    return np.random.permutation(T)[(T * np.random.uniform(0, 1, S) ** 4).astype(np.int64)]


T, S, P, K, K2, H, N = 2048, 1024, 512, 1024, 512, 1024, 384

def setup_inputs():
    n = np.random.standard_normal
    s, s2, u = mx_kscale(K)[:, None], mx_kscale(K2)[:, None], mx_kscale(H)[:, None]
    d = {}
    d["tab_words"], d["tab_scales"] = pack_weight(n((K, T)) * s, "e4m3")
    d["tab2_words"], d["tab2_scales"] = pack_weight(n((K2, T)) * s2, "e4m3")
    d["tab3_words"], d["tab3_scales"] = pack_weight(n((K2, T)) * s2, "e4m3")
    d["offs"] = striped(np.random.permutation(T)[:S])
    d["offs2"] = striped(np.random.permutation(T)[:S])
    d["offs3"] = striped(np.random.permutation(T)[:S])
    d["pos1"] = striped(np.random.permutation(S)[:P])
    d["pos2"] = striped(often(S, P))
    d["pos3"] = striped(often(S, P))
    d["w1"] = (n((K, H)) / K ** 0.5 / s * u.T).astype(np.float32)
    d["w2_words"], d["w2_scales"] = pack_weight(n((K2, H)) / K2 ** 0.5 / s2, "e2m1")
    d["w3"] = (n((K2, H)) / K2 ** 0.5 / s2 * u.T).astype(np.float32)
    d["w4_words"], d["w4_scales"] = pack_weight(n((H, N)) / H ** 0.5 / u, "e2m1")
    d["w5"] = (n((H, N)) / H ** 0.5 / u).astype(np.float32)
    d["room"] = n((N, P)).astype(np.float32)
    return d

def reference(tab_words, tab_scales, tab2_words, tab2_scales, tab3_words, tab3_scales,
              offs, offs2, offs3, pos1, pos2, pos3,
              w1, w2_words, w2_scales, w3, w4_words, w4_scales, w5, room):
    v = unpack_weight(tab_words, tab_scales, "e4m3")[:, unstriped(offs)]
    v2 = unpack_weight(tab2_words, tab2_scales, "e4m3")[:, unstriped(offs2)]
    v3 = unpack_weight(tab3_words, tab3_scales, "e4m3")[:, unstriped(offs3)]
    a = mxq(f64(w1), 0, "e4m3").T @ v
    b = unpack_weight(w2_words, w2_scales, "e2m1").T @ v2
    d = mxq(f64(w3), 0, "e4m3").T @ v3
    aw = a[:, unstriped(pos1)]
    bw = b[:, unstriped(pos2)]
    dw = d[:, unstriped(pos3)]
    z = mxq(np.maximum(aw, dw) * bw + np.minimum(aw, dw), 0, "e4m3")
    y4 = unpack_weight(w4_words, w4_scales, "e2m1").T @ z
    y5 = mxq(f64(w5), 0, "e4m3").T @ z
    return y4 / (1.0 + np.exp(-y4)) + f64(room) * y5

@@ -1,0 +1,239 @@
+from contextlib import ExitStack
+
+import concourse.mybir as mybir
+
+T, S, NW, K, K2, H, N = 2048, 1024, 512, 1024, 512, 1024, 384
+FLOPS = 2 * (K * H * S + 2 * K2 * H * S + 2 * H * N * NW)
+
+F32 = mybir.dt.float32
+BF16 = mybir.dt.bfloat16
+I32 = mybir.dt.int32
+U32 = mybir.dt.uint32
+U16 = mybir.dt.uint16
+U8 = mybir.dt.uint8
+FP8X4 = mybir.dt.float8_e4m3fn_x4
+FP4X4 = mybir.dt.float4_e2m1fn_x4
+ALU = mybir.AluOpType
+ACT = mybir.ActivationFunctionType
+
+P = 128
+PACK = 4
+K_PASS = P * PACK
+BANK = 512
+
+
+def tile_list_clinic_triage_join_kernel(
+    tc, tab_words, tab_scales, tab2_words, tab2_scales, tab3_words, tab3_scales,
+    offs, offs2, offs3, pos1, pos2, pos3,
+    w1, w2_words, w2_scales, w3, w4_words, w4_scales, w5, room, out,
+):
+    nc = tc.nc
+    with ExitStack() as ctx:
+        lists = ctx.enter_context(tc.tile_pool(name="lists", bufs=1))
+        keep = ctx.enter_context(tc.tile_pool(name="keep", bufs=1))
+        ring = ctx.enter_context(tc.tile_pool(name="ring", bufs=1))
+        psum = ctx.enter_context(tc.psum_pool(name="psum", bufs=8))
+
+        def load_list(src, name):
+            tile = lists.tile(list(src.shape), U16, name=name)
+            nc.sync.dma_start(tile[:], src)
+            return tile
+
+        def zeroed_plane(shape, name):
+            plane = keep.tile(shape, U8, name=name, align_bytes=64)
+            flat = plane[:] if len(shape) == 2 else plane[:].rearrange("p a n -> p (a n)")
+            nc.vector.memset(flat.bitcast(I32), 0)
+            return plane
+
+        def load_words(words, a, name):
+            tile = keep.tile([P, T], I32, name=name, align_bytes=64)
+            nc.sync.dma_start(tile[:], words[a].rearrange("p t i -> p (t i)").bitcast(I32))
+            return tile
+
+        def load_scale_rows(plane, scales):
+            rows = 4 * scales.shape[0]
+            for q in range(4):
+                nc.sync.dma_start(
+                    plane[32 * q : 32 * q + rows, :].bitcast(I32),
+                    scales[:, 4 * q : 4 * q + 4, :].bitcast(I32),
+                )
+
+        def load_rows(w, a, cols, name):
+            width = cols.stop - cols.start
+            raw = ring.tile([P, PACK, width], F32, name=name, tag="raw", bufs=6)
+            nc.sync.dma_start(raw[:], w[a * K_PASS : (a + 1) * K_PASS, cols].rearrange("(p i) c -> p i c", i=PACK))
+            return raw
+
+        def gather(table, offsets, dtype, name):
+            picked = keep.tile([P, S], dtype, name=name, align_bytes=64)
+            nc.vector.tensor_copy(picked[:], table[:].bitcast(dtype).indirect(offsets[:]))
+            return picked
+
+        def gather_bytes(table, offsets, name):
+            picked = keep.tile([P, S], U8, name=name, align_bytes=64)
+            nc.vector.tensor_copy(picked[:], table[:].indirect(offsets[:]))
+            return picked
+
+        def round_and_deal(raw, name):
+            grouped = ring.tile([P, PACK, P, PACK], BF16, name=name, tag="grouped", bufs=3, align_bytes=64)
+            nc.scalar.copy(grouped[:].rearrange("p t m i -> p m t i"), raw[:].rearrange("p i (m t) -> p m t i", t=PACK))
+            return grouped
+
+        def quantise(flat, name):
+            width = flat.shape[1] // PACK
+            codes = keep.tile([P, width], U32, name=name + "_codes", align_bytes=64)
+            plane = keep.tile([P, width], U8, name=name + "_plane", align_bytes=64)
+            nc.vector.quantize_mx(out=codes[:].bitcast(FP8X4), scales=plane[:], in_=flat)
+            return codes, plane
+
+        w2_plane_raw = zeroed_plane([P, H], "w2_plane_raw")
+        tab3_plane = zeroed_plane([P, T], "tab3_plane")
+        tab_plane = zeroed_plane([P, T], "tab_plane")
+        tab2_plane = zeroed_plane([P, T], "tab2_plane")
+        w4_plane = zeroed_plane([P, 2, N], "w4_plane")
+
+        half = [slice(b * K_PASS, (b + 1) * K_PASS) for b in range(2)]
+        w2_raw = keep.tile([P, 2 * H], U8, name="w2_raw", align_bytes=64)
+        nc.sync.dma_start(w2_raw[:].bitcast(I32), w2_words[0].bitcast(I32))
+        offs3_t = load_list(offs3, "offs3_t")
+        tab3_t = load_words(tab3_words, 0, "tab3_t")
+        load_scale_rows(w2_plane_raw, w2_scales)
+        tab_t = [load_words(tab_words, 0, "tab_t0")]
+        load_scale_rows(tab3_plane, tab3_scales)
+        offs_t = load_list(offs, "offs_t")
+        tab_t.append(load_words(tab_words, 1, "tab_t1"))
+        load_scale_rows(tab_plane, tab_scales)
+        w1_raw = {(0, a): load_rows(w1, a, half[0], "w1_raw0%d" % a) for a in range(2)}
+        w3_raw = {0: load_rows(w3, 0, half[0], "w3_raw0")}
+        offs2_t = load_list(offs2, "offs2_t")
+        tab2_t = load_words(tab2_words, 0, "tab2_t")
+        load_scale_rows(tab2_plane, tab2_scales)
+        pos1_t = load_list(pos1, "pos1_t")
+        pos3_t = load_list(pos3, "pos3_t")
+        pos2_t = load_list(pos2, "pos2_t")
+        for a in range(2):
+            w1_raw[(1, a)] = load_rows(w1, a, half[1], "w1_raw1%d" % a)
+        w3_raw[1] = load_rows(w3, 0, half[1], "w3_raw1")
+        w5_raw = [load_rows(w5, a, slice(0, N), "w5_raw%d" % a) for a in range(2)]
+        w4_t = keep.tile([P, 2, 2 * N], U8, name="w4_t", align_bytes=64)
+        nc.sync.dma_start(w4_t[:].bitcast(I32), w4_words.rearrange("a p n -> p a n").bitcast(I32))
+        for q in range(4):
+            nc.sync.dma_start(
+                w4_plane[32 * q : 32 * q + 4, :, :].bitcast(I32),
+                w4_scales[:, 4 * q : 4 * q + 4, :].rearrange("a r n -> r a n").bitcast(I32),
+            )
+        room_t = ring.tile([P, 3, NW], F32, name="room_t", tag="raw", bufs=6)
+        nc.sync.dma_start(room_t[:], room.rearrange("(c p) j -> p c j", p=P))
+
+        w2_t = keep.tile([P, 2 * H], U8, name="w2_t", align_bytes=64)
+        nc.vector.tensor_copy(
+            w2_t[:].rearrange("p (b t m e) -> p b t m e", b=2, t=PACK, e=2),
+            w2_raw[:].rearrange("p (b m t e) -> p b t m e", b=2, t=PACK, e=2),
+        )
+        w2_plane = keep.tile([P, H], U8, name="w2_plane", align_bytes=64)
+        nc.vector.tensor_copy(
+            w2_plane[:].rearrange("p (b t m) -> p b t m", b=2, t=PACK),
+            w2_plane_raw[:].rearrange("p (b m t) -> p b t m", b=2, t=PACK),
+        )
+
+        v3 = gather(tab3_t, offs3_t, U32, "v3")
+        v3_plane = gather_bytes(tab3_plane, offs3_t, "v3_plane")
+        v = [gather(tab_t[a], offs_t, U32, "v_%d" % a) for a in range(2)]
+        v_plane = gather_bytes(tab_plane, offs_t, "v_plane")
+
+        def flat(grouped):
+            return grouped[:].rearrange("p t m i -> p (t m i)")
+
+        w1_q, w3_q = {}, {}
+
+        def prepare_weights(b):
+            for a in range(2):
+                w1_q[(b, a)] = quantise(flat(round_and_deal(w1_raw[(b, a)], "w1_g%d%d" % (b, a))), "w1_q%d%d" % (b, a))
+            w3_q[b] = quantise(flat(round_and_deal(w3_raw[b], "w3_g%d" % b)), "w3_q%d" % b)
+
+        prepare_weights(0)
+        v2 = gather(tab2_t, offs2_t, U32, "v2")
+        v2_plane = gather_bytes(tab2_plane, offs2_t, "v2_plane")
+
+        def first_stage(passes, tag, s):
+            window = ring.tile([P, S], F32, name="%s_win%d" % (tag, s), tag=tag, bufs=3)
+            for h in range(2):
+                cols = slice(h * BANK, (h + 1) * BANK)
+                acc = psum.tile([P, BANK], F32, name="acc", tag="acc")
+                for i, (lhs, lhs_scale, rhs, rhs_plane, k) in enumerate(passes):
+                    nc.tensor.matmul_mx(
+                        out=acc[:], lhsT=lhs, lhsT_scale=lhs_scale,
+                        rhs=rhs[:, cols].bitcast(FP8X4), rhs_scale=rhs_plane[k:P, cols],
+                        start=(i == 0), stop=(i == len(passes) - 1),
+                    )
+                nc.scalar.copy(window[:, cols], acc[:])
+            return window
+
+        z_q = []
+        for b in range(2):
+            larger_b = ring.tile([P, PACK, NW], F32, name="larger_b", tag="larger_b")
+            smaller = ring.tile([P, PACK, NW], F32, name="smaller", tag="smaller")
+            for t in range(PACK):
+                s = PACK * b + t
+                m = slice(t * P, (t + 1) * P)
+                a_win = first_stage(
+                    [(w1_q[(b, a)][0][:, m].bitcast(FP8X4), w1_q[(b, a)][1][:, m], v[a], v_plane, 4 * a) for a in range(2)],
+                    "a", s)
+                d_win = first_stage([(w3_q[b][0][:, m].bitcast(FP8X4), w3_q[b][1][:, m], v3, v3_plane, 0)], "d", s)
+                b_win = first_stage(
+                    [(w2_t[:, 2 * s * P : 2 * (s + 1) * P].bitcast(FP4X4), w2_plane[:, s * P : (s + 1) * P], v2, v2_plane, 0)],
+                    "b", s)
+                aw = ring.tile([P, NW], F32, name="aw", tag="aw", bufs=2)
+                dw = ring.tile([P, NW], F32, name="dw", tag="dw", bufs=2)
+                larger = ring.tile([P, NW], F32, name="larger", tag="larger", bufs=2)
+                nc.vector.tensor_copy(aw[:], a_win[:].indirect(pos1_t[:]))
+                nc.vector.tensor_copy(dw[:], d_win[:].indirect(pos3_t[:]))
+                nc.vector.tensor_tensor(larger[:], aw[:], dw[:], ALU.max)
+                nc.vector.tensor_tensor(smaller[:, t, :], aw[:], dw[:], ALU.min)
+                nc.vector.tensor_tensor(larger_b[:, t, :], b_win[:].indirect(pos2_t[:]), larger[:], ALU.mult)
+                if s == 1:
+                    prepare_weights(1)
+                if s == 4:
+                    w5_g = ring.tile([P, 2, N, PACK], BF16, name="w5_g", tag="w5_g", align_bytes=64)
+                    for a in range(2):
+                        nc.scalar.copy(
+                            w5_g[:, a].rearrange("p (c k) i -> p c i k", k=4),
+                            w5_raw[a][:].rearrange("p i (c k) -> p c i k", k=4),
+                        )
+                    w5_flat = w5_g[:].rearrange("p a n i -> p (a n i)")
+                    w5_codes = keep.tile([P, 2 * N], U32, name="w5_codes", align_bytes=64)
+                    w5_plane = keep.tile([P, 2 * N], U8, name="w5_plane", align_bytes=64)
+                    for c0, c1 in ((0, 512), (512, 2 * N)):
+                        nc.vector.quantize_mx(
+                            out=w5_codes[:, c0:c1].bitcast(FP8X4), scales=w5_plane[:, c0:c1],
+                            in_=w5_flat[:, PACK * c0 : PACK * c1])
+            z = ring.tile([P, NW, PACK], BF16, name="z", tag="grouped", bufs=3, align_bytes=64)
+            nc.vector.tensor_tensor(
+                z[:].rearrange("p (c i) t -> p c t i", i=2),
+                larger_b[:].rearrange("p t (c i) -> p c t i", i=2),
+                smaller[:].rearrange("p t (c i) -> p c t i", i=2),
+                ALU.add,
+            )
+            z_q.append(quantise(z[:].rearrange("p j t -> p (j t)"), "z%d" % b))
+
+        y4 = [psum.tile([P, NW], F32, name="y4_%d" % c, tag="acc") for c in range(3)]
+        y5 = [psum.tile([P, NW], F32, name="y5_%d" % c, tag="acc") for c in range(3)]
+        for b in range(2):
+            z_codes, z_plane = z_q[b]
+            for c in range(3):
+                cols = slice(b * N + c * P, b * N + (c + 1) * P)
+                nc.tensor.matmul_mx(
+                    out=y5[c][:], lhsT=w5_codes[:, cols].bitcast(FP8X4), lhsT_scale=w5_plane[:, cols],
+                    rhs=z_codes[:].bitcast(FP8X4), rhs_scale=z_plane[:], start=(b == 0), stop=(b == 1))
+                nc.tensor.matmul_mx(
+                    out=y4[c][:], lhsT=w4_t[:, b, 2 * c * P : 2 * (c + 1) * P].bitcast(FP4X4),
+                    lhsT_scale=w4_plane[:, b, c * P : (c + 1) * P],
+                    rhs=z_codes[:].bitcast(FP8X4), rhs_scale=z_plane[:], start=(b == 0), stop=(b == 1))
+        for c in range(3):
+            gated = ring.tile([P, NW], F32, name="gated", tag="a", bufs=3)
+            weighted = ring.tile([P, NW], F32, name="weighted", tag="d", bufs=3)
+            result = ring.tile([P, NW], F32, name="result", tag="b", bufs=3)
+            nc.scalar.activation(gated[:], y4[c][:], ACT.Silu)
+            nc.vector.tensor_tensor(weighted[:], y5[c][:], room_t[:, c, :], ALU.mult)
+            nc.vector.tensor_tensor(result[:], gated[:], weighted[:], ALU.add)
+            nc.sync.dma_start(out[c * P : (c + 1) * P, :], result[:])

@@ -39,10 +39,10 @@ def tile_list_clinic_triage_join_kernel(
             nc.sync.dma_start(tile[:], src)
             return tile
 
-        def zeroed_plane(shape, name):
+        def zeroed_plane(shape, name, engine):
             plane = keep.tile(shape, U8, name=name, align_bytes=64)
             flat = plane[:] if len(shape) == 2 else plane[:].rearrange("p a n -> p (a n)")
-            nc.vector.memset(flat.bitcast(I32), 0)
+            engine.memset(flat.bitcast(I32), 0)
             return plane
 
         def load_words(words, a, name):
@@ -86,34 +86,34 @@ def tile_list_clinic_triage_join_kernel(
             nc.vector.quantize_mx(out=codes[:].bitcast(FP8X4), scales=plane[:], in_=flat)
             return codes, plane
 
-        w2_plane_raw = zeroed_plane([P, H], "w2_plane_raw")
-        tab3_plane = zeroed_plane([P, T], "tab3_plane")
-        tab_plane = zeroed_plane([P, T], "tab_plane")
-        tab2_plane = zeroed_plane([P, T], "tab2_plane")
-        w4_plane = zeroed_plane([P, 2, N], "w4_plane")
+        tab3_plane = zeroed_plane([P, T], "tab3_plane", nc.vector)
+        tab_plane = zeroed_plane([P, T], "tab_plane", nc.gpsimd)
+        w2_plane_raw = zeroed_plane([P, H], "w2_plane_raw", nc.vector)
+        tab2_plane = zeroed_plane([P, T], "tab2_plane", nc.gpsimd)
+        w4_plane = zeroed_plane([P, 2, N], "w4_plane", nc.gpsimd)
 
         half = [slice(b * K_PASS, (b + 1) * K_PASS) for b in range(2)]
         w2_raw = keep.tile([P, 2 * H], U8, name="w2_raw", align_bytes=64)
         nc.sync.dma_start(w2_raw[:].bitcast(I32), w2_words[0].bitcast(I32))
         offs3_t = load_list(offs3, "offs3_t")
-        tab3_t = load_words(tab3_words, 0, "tab3_t")
-        load_scale_rows(w2_plane_raw, w2_scales)
-        tab_t = [load_words(tab_words, 0, "tab_t0")]
         load_scale_rows(tab3_plane, tab3_scales)
-        offs_t = load_list(offs, "offs_t")
-        tab_t.append(load_words(tab_words, 1, "tab_t1"))
-        load_scale_rows(tab_plane, tab_scales)
-        w1_raw = {(0, a): load_rows(w1, a, half[0], "w1_raw0%d" % a) for a in range(2)}
+        tab3_t = load_words(tab3_words, 0, "tab3_t")
         w3_raw = {0: load_rows(w3, 0, half[0], "w3_raw0")}
+        offs_t = load_list(offs, "offs_t")
+        load_scale_rows(tab_plane, tab_scales)
+        tab_t = [load_words(tab_words, 0, "tab_t0")]
+        load_scale_rows(w2_plane_raw, w2_scales)
+        tab_t.append(load_words(tab_words, 1, "tab_t1"))
         offs2_t = load_list(offs2, "offs2_t")
-        tab2_t = load_words(tab2_words, 0, "tab2_t")
         load_scale_rows(tab2_plane, tab2_scales)
+        w1_raw = {(0, a): load_rows(w1, a, half[0], "w1_raw0%d" % a) for a in range(2)}
+        tab2_t = load_words(tab2_words, 0, "tab2_t")
         pos1_t = load_list(pos1, "pos1_t")
         pos3_t = load_list(pos3, "pos3_t")
         pos2_t = load_list(pos2, "pos2_t")
+        w3_raw[1] = load_rows(w3, 0, half[1], "w3_raw1")
         for a in range(2):
             w1_raw[(1, a)] = load_rows(w1, a, half[1], "w1_raw1%d" % a)
-        w3_raw[1] = load_rows(w3, 0, half[1], "w3_raw1")
         w5_raw = [load_rows(w5, a, slice(0, N), "w5_raw%d" % a) for a in range(2)]
         w4_t = keep.tile([P, 2, 2 * N], U8, name="w4_t", align_bytes=64)
         nc.sync.dma_start(w4_t[:].bitcast(I32), w4_words.rearrange("a p n -> p a n").bitcast(I32))
@@ -127,8 +127,8 @@ def tile_list_clinic_triage_join_kernel(
 
         w2_t = keep.tile([P, 2 * H], U8, name="w2_t", align_bytes=64)
         nc.vector.tensor_copy(
-            w2_t[:].rearrange("p (b t m e) -> p b t m e", b=2, t=PACK, e=2),
-            w2_raw[:].rearrange("p (b m t e) -> p b t m e", b=2, t=PACK, e=2),
+            w2_t[:].bitcast(U16).rearrange("p (b t m) -> p b t m", b=2, t=PACK),
+            w2_raw[:].bitcast(U16).rearrange("p (b m t) -> p b t m", b=2, t=PACK),
         )
         w2_plane = keep.tile([P, H], U8, name="w2_plane", align_bytes=64)
         nc.vector.tensor_copy(
@@ -136,27 +136,19 @@ def tile_list_clinic_triage_join_kernel(
             w2_plane_raw[:].rearrange("p (b m t) -> p b t m", b=2, t=PACK),
         )
 
-        v3 = gather(tab3_t, offs3_t, U32, "v3")
-        v3_plane = gather_bytes(tab3_plane, offs3_t, "v3_plane")
-        v = [gather(tab_t[a], offs_t, U32, "v_%d" % a) for a in range(2)]
-        v_plane = gather_bytes(tab_plane, offs_t, "v_plane")
-
         def flat(grouped):
             return grouped[:].rearrange("p t m i -> p (t m i)")
 
         w1_q, w3_q = {}, {}
 
-        def prepare_weights(b):
-            for a in range(2):
-                w1_q[(b, a)] = quantise(flat(round_and_deal(w1_raw[(b, a)], "w1_g%d%d" % (b, a))), "w1_q%d%d" % (b, a))
+        def prepare_w1(b, a):
+            w1_q[(b, a)] = quantise(flat(round_and_deal(w1_raw[(b, a)], "w1_g%d%d" % (b, a))), "w1_q%d%d" % (b, a))
+
+        def prepare_w3(b):
             w3_q[b] = quantise(flat(round_and_deal(w3_raw[b], "w3_g%d" % b)), "w3_q%d" % b)
 
-        prepare_weights(0)
-        v2 = gather(tab2_t, offs2_t, U32, "v2")
-        v2_plane = gather_bytes(tab2_plane, offs2_t, "v2_plane")
-
         def first_stage(passes, tag, s):
-            window = ring.tile([P, S], F32, name="%s_win%d" % (tag, s), tag=tag, bufs=3)
+            window = ring.tile([P, S], F32, name="%s_win%d" % (tag, s), tag=tag, bufs=4)
             for h in range(2):
                 cols = slice(h * BANK, (h + 1) * BANK)
                 acc = psum.tile([P, BANK], F32, name="acc", tag="acc")
@@ -169,52 +161,83 @@ def tile_list_clinic_triage_join_kernel(
                 nc.scalar.copy(window[:, cols], acc[:])
             return window
 
-        z_q = []
-        for b in range(2):
-            larger_b = ring.tile([P, PACK, NW], F32, name="larger_b", tag="larger_b")
-            smaller = ring.tile([P, PACK, NW], F32, name="smaller", tag="smaller")
-            for t in range(PACK):
-                s = PACK * b + t
-                m = slice(t * P, (t + 1) * P)
-                a_win = first_stage(
-                    [(w1_q[(b, a)][0][:, m].bitcast(FP8X4), w1_q[(b, a)][1][:, m], v[a], v_plane, 4 * a) for a in range(2)],
-                    "a", s)
-                d_win = first_stage([(w3_q[b][0][:, m].bitcast(FP8X4), w3_q[b][1][:, m], v3, v3_plane, 0)], "d", s)
-                b_win = first_stage(
-                    [(w2_t[:, 2 * s * P : 2 * (s + 1) * P].bitcast(FP4X4), w2_plane[:, s * P : (s + 1) * P], v2, v2_plane, 0)],
-                    "b", s)
-                aw = ring.tile([P, NW], F32, name="aw", tag="aw", bufs=2)
-                dw = ring.tile([P, NW], F32, name="dw", tag="dw", bufs=2)
-                larger = ring.tile([P, NW], F32, name="larger", tag="larger", bufs=2)
-                nc.vector.tensor_copy(aw[:], a_win[:].indirect(pos1_t[:]))
-                nc.vector.tensor_copy(dw[:], d_win[:].indirect(pos3_t[:]))
-                nc.vector.tensor_tensor(larger[:], aw[:], dw[:], ALU.max)
-                nc.vector.tensor_tensor(smaller[:, t, :], aw[:], dw[:], ALU.min)
-                nc.vector.tensor_tensor(larger_b[:, t, :], b_win[:].indirect(pos2_t[:]), larger[:], ALU.mult)
-                if s == 1:
-                    prepare_weights(1)
-                if s == 4:
-                    w5_g = ring.tile([P, 2, N, PACK], BF16, name="w5_g", tag="w5_g", align_bytes=64)
-                    for a in range(2):
-                        nc.scalar.copy(
-                            w5_g[:, a].rearrange("p (c k) i -> p c i k", k=4),
-                            w5_raw[a][:].rearrange("p i (c k) -> p c i k", k=4),
-                        )
-                    w5_flat = w5_g[:].rearrange("p a n i -> p (a n i)")
-                    w5_codes = keep.tile([P, 2 * N], U32, name="w5_codes", align_bytes=64)
-                    w5_plane = keep.tile([P, 2 * N], U8, name="w5_plane", align_bytes=64)
-                    for c0, c1 in ((0, 512), (512, 2 * N)):
-                        nc.vector.quantize_mx(
-                            out=w5_codes[:, c0:c1].bitcast(FP8X4), scales=w5_plane[:, c0:c1],
-                            in_=w5_flat[:, PACK * c0 : PACK * c1])
+        def a_rows(s):
+            b, t = divmod(s, PACK)
+            m = slice(t * P, (t + 1) * P)
+            return first_stage(
+                [(w1_q[(b, a)][0][:, m].bitcast(FP8X4), w1_q[(b, a)][1][:, m], v[a], v_plane, 4 * a) for a in range(2)],
+                "a", s)
+
+        def d_rows(s):
+            b, t = divmod(s, PACK)
+            m = slice(t * P, (t + 1) * P)
+            return first_stage([(w3_q[b][0][:, m].bitcast(FP8X4), w3_q[b][1][:, m], v3, v3_plane, 0)], "d", s)
+
+        def b_rows(s):
+            return first_stage(
+                [(w2_t[:, 2 * s * P : 2 * (s + 1) * P].bitcast(FP4X4), w2_plane[:, s * P : (s + 1) * P], v2, v2_plane, 0)],
+                "b", s)
+
+        v3_plane = gather_bytes(tab3_plane, offs3_t, "v3_plane")
+        v3 = gather(tab3_t, offs3_t, U32, "v3")
+        prepare_w3(0)
+        d_wins = {s: d_rows(s) for s in range(PACK)}
+        v_plane = gather_bytes(tab_plane, offs_t, "v_plane")
+        v = [gather(tab_t[a], offs_t, U32, "v_%d" % a) for a in range(2)]
+        v2_plane = gather_bytes(tab2_plane, offs2_t, "v2_plane")
+        prepare_w1(0, 0)
+        prepare_w1(0, 1)
+        v2 = gather(tab2_t, offs2_t, U32, "v2")
+
+        def prepare_w5():
+            w5_g = ring.tile([P, 2, N, PACK], BF16, name="w5_g", tag="w5_g", align_bytes=64)
+            for a in range(2):
+                nc.scalar.copy(
+                    w5_g[:, a].rearrange("p (c k) i -> p c i k", k=4),
+                    w5_raw[a][:].rearrange("p i (c k) -> p c i k", k=4),
+                )
+            w5_flat = w5_g[:].rearrange("p a n i -> p (a n i)")
+            for c0, c1 in ((0, 512), (512, 2 * N)):
+                nc.vector.quantize_mx(
+                    out=w5_codes[:, c0:c1].bitcast(FP8X4), scales=w5_plane[:, c0:c1],
+                    in_=w5_flat[:, PACK * c0 : PACK * c1])
+
+        def weave_and_quantise(b, weave):
             z = ring.tile([P, NW, PACK], BF16, name="z", tag="grouped", bufs=3, align_bytes=64)
-            nc.vector.tensor_tensor(
-                z[:].rearrange("p (c i) t -> p c t i", i=2),
-                larger_b[:].rearrange("p t (c i) -> p c t i", i=2),
-                smaller[:].rearrange("p t (c i) -> p c t i", i=2),
-                ALU.add,
-            )
-            z_q.append(quantise(z[:].rearrange("p j t -> p (j t)"), "z%d" % b))
+            weave(z[:].rearrange("p (c i) t -> p c t i", i=4), z_rows[b][:].rearrange("p t (c i) -> p c t i", i=4))
+            return quantise(z[:].rearrange("p j t -> p (j t)"), "z%d" % b)
+
+        w5_codes = keep.tile([P, 2 * N], U32, name="w5_codes", align_bytes=64)
+        w5_plane = keep.tile([P, 2 * N], U8, name="w5_plane", align_bytes=64)
+        z_rows = [keep.tile([P, PACK, NW], BF16, name="z_rows%d" % b) for b in range(2)]
+        z_q = []
+        for s in range(2 * PACK):
+            b, t = divmod(s, PACK)
+            d_win = d_wins[s] if b == 0 else d_rows(s)
+            a_win = a_rows(s)
+            b_win = b_rows(s)
+            aw = ring.tile([P, NW], F32, name="aw", tag="aw", bufs=2)
+            dw = ring.tile([P, NW], F32, name="dw", tag="dw", bufs=2)
+            larger = ring.tile([P, NW], F32, name="larger", tag="larger", bufs=2)
+            smaller = ring.tile([P, NW], F32, name="smaller", tag="smaller", bufs=2)
+            product = ring.tile([P, NW], F32, name="product", tag="product", bufs=2)
+            nc.vector.tensor_copy(dw[:], d_win[:].indirect(pos3_t[:]))
+            nc.vector.tensor_copy(aw[:], a_win[:].indirect(pos1_t[:]))
+            nc.vector.tensor_tensor(larger[:], aw[:], dw[:], ALU.max)
+            nc.vector.tensor_tensor(smaller[:], aw[:], dw[:], ALU.min)
+            nc.vector.tensor_tensor(product[:], b_win[:].indirect(pos2_t[:]), larger[:], ALU.mult)
+            adder = nc.vector if s == 2 * PACK - 1 else nc.gpsimd
+            adder.tensor_tensor(z_rows[b][:, t, :], product[:], smaller[:], ALU.add)
+            if s == 2:
+                prepare_w3(1)
+                prepare_w1(1, 0)
+            if s == 3:
+                prepare_w1(1, 1)
+            if s == 5:
+                z_q.append(weave_and_quantise(0, nc.scalar.copy))
+            if s == 6:
+                prepare_w5()
+        z_q.append(weave_and_quantise(1, nc.vector.tensor_copy))
 
         y4 = [psum.tile([P, NW], F32, name="y4_%d" % c, tag="acc") for c in range(3)]
         y5 = [psum.tile([P, NW], F32, name="y5_%d" % c, tag="acc") for c in range(3)]
@@ -230,9 +253,9 @@ def tile_list_clinic_triage_join_kernel(
                     lhsT_scale=w4_plane[:, b, c * P : (c + 1) * P],
                     rhs=z_codes[:].bitcast(FP8X4), rhs_scale=z_plane[:], start=(b == 0), stop=(b == 1))
         for c in range(3):
-            gated = ring.tile([P, NW], F32, name="gated", tag="a", bufs=3)
-            weighted = ring.tile([P, NW], F32, name="weighted", tag="d", bufs=3)
-            result = ring.tile([P, NW], F32, name="result", tag="b", bufs=3)
+            gated = ring.tile([P, NW], F32, name="gated", tag="a", bufs=4)
+            weighted = ring.tile([P, NW], F32, name="weighted", tag="d", bufs=4)
+            result = ring.tile([P, NW], F32, name="result", tag="b", bufs=4)
             nc.scalar.activation(gated[:], y4[c][:], ACT.Silu)
             nc.vector.tensor_tensor(weighted[:], y5[c][:], room_t[:, c, :], ALU.mult)
             nc.vector.tensor_tensor(result[:], gated[:], weighted[:], ALU.add)

@@ -51,12 +51,15 @@ def tile_list_clinic_triage_join_kernel(
             return tile
 
         def load_scale_rows(plane, scales):
-            rows = 4 * scales.shape[0]
-            for q in range(4):
-                nc.sync.dma_start(
-                    plane[32 * q : 32 * q + rows, :].bitcast(I32),
-                    scales[:, 4 * q : 4 * q + 4, :].bitcast(I32),
-                )
+            if scales.shape[0] == 2:
+                for q in range(4):
+                    nc.sync.dma_start(
+                        plane[32 * q : 32 * q + 8, :].bitcast(I32),
+                        scales[:, 4 * q : 4 * q + 4, :].bitcast(I32),
+                    )
+            else:
+                for r in range(4):
+                    nc.sync.dma_start(plane[r:P:32, :].bitcast(I32), scales[0, r:16:4, :].bitcast(I32))
 
         def load_rows(w, a, cols, name):
             width = cols.stop - cols.start
@@ -99,28 +102,28 @@ def tile_list_clinic_triage_join_kernel(
         load_scale_rows(tab3_plane, tab3_scales)
         tab3_t = load_words(tab3_words, 0, "tab3_t")
         w3_raw = {0: load_rows(w3, 0, half[0], "w3_raw0")}
+        pos3_t = load_list(pos3, "pos3_t")
         offs_t = load_list(offs, "offs_t")
         load_scale_rows(tab_plane, tab_scales)
-        tab_t = [load_words(tab_words, 0, "tab_t0")]
-        load_scale_rows(w2_plane_raw, w2_scales)
-        tab_t.append(load_words(tab_words, 1, "tab_t1"))
+        tab_t = [load_words(tab_words, a, "tab_t%d" % a) for a in range(2)]
         offs2_t = load_list(offs2, "offs2_t")
         load_scale_rows(tab2_plane, tab2_scales)
-        w1_raw = {(0, a): load_rows(w1, a, half[0], "w1_raw0%d" % a) for a in range(2)}
-        tab2_t = load_words(tab2_words, 0, "tab2_t")
+        w1_raw = {(0, 0): load_rows(w1, 0, half[0], "w1_raw00")}
+        load_scale_rows(w2_plane_raw, w2_scales)
+        w1_raw[(0, 1)] = load_rows(w1, 1, half[0], "w1_raw01")
         pos1_t = load_list(pos1, "pos1_t")
-        pos3_t = load_list(pos3, "pos3_t")
         pos2_t = load_list(pos2, "pos2_t")
+        tab2_t = load_words(tab2_words, 0, "tab2_t")
         w3_raw[1] = load_rows(w3, 0, half[1], "w3_raw1")
         for a in range(2):
             w1_raw[(1, a)] = load_rows(w1, a, half[1], "w1_raw1%d" % a)
         w5_raw = [load_rows(w5, a, slice(0, N), "w5_raw%d" % a) for a in range(2)]
         w4_t = keep.tile([P, 2, 2 * N], U8, name="w4_t", align_bytes=64)
         nc.sync.dma_start(w4_t[:].bitcast(I32), w4_words.rearrange("a p n -> p a n").bitcast(I32))
-        for q in range(4):
+        for r in range(4):
             nc.sync.dma_start(
-                w4_plane[32 * q : 32 * q + 4, :, :].bitcast(I32),
-                w4_scales[:, 4 * q : 4 * q + 4, :].rearrange("a r n -> r a n").bitcast(I32),
+                w4_plane[r:P:32, :, :].bitcast(I32),
+                w4_scales[:, r:16:4, :].rearrange("a q n -> q a n").bitcast(I32),
             )
         room_t = ring.tile([P, 3, NW], F32, name="room_t", tag="raw", bufs=6)
         nc.sync.dma_start(room_t[:], room.rearrange("(c p) j -> p c j", p=P))
@@ -178,15 +181,21 @@ def tile_list_clinic_triage_join_kernel(
                 [(w2_t[:, 2 * s * P : 2 * (s + 1) * P].bitcast(FP4X4), w2_plane[:, s * P : (s + 1) * P], v2, v2_plane, 0)],
                 "b", s)
 
+        def pick_d(d_win):
+            dw = ring.tile([P, NW], F32, name="dw", tag="dw", bufs=4)
+            nc.vector.tensor_copy(dw[:], d_win[:].indirect(pos3_t[:]))
+            return dw
+
         v3_plane = gather_bytes(tab3_plane, offs3_t, "v3_plane")
         v3 = gather(tab3_t, offs3_t, U32, "v3")
         prepare_w3(0)
         d_wins = {s: d_rows(s) for s in range(PACK)}
         v_plane = gather_bytes(tab_plane, offs_t, "v_plane")
         v = [gather(tab_t[a], offs_t, U32, "v_%d" % a) for a in range(2)]
-        v2_plane = gather_bytes(tab2_plane, offs2_t, "v2_plane")
         prepare_w1(0, 0)
         prepare_w1(0, 1)
+        dws = {s: pick_d(d_wins[s]) for s in range(PACK)}
+        v2_plane = gather_bytes(tab2_plane, offs2_t, "v2_plane")
         v2 = gather(tab2_t, offs2_t, U32, "v2")
 
         def prepare_w5():
@@ -213,15 +222,13 @@ def tile_list_clinic_triage_join_kernel(
         z_q = []
         for s in range(2 * PACK):
             b, t = divmod(s, PACK)
-            d_win = d_wins[s] if b == 0 else d_rows(s)
+            dw = dws[s] if b == 0 else pick_d(d_rows(s))
             a_win = a_rows(s)
             b_win = b_rows(s)
             aw = ring.tile([P, NW], F32, name="aw", tag="aw", bufs=2)
-            dw = ring.tile([P, NW], F32, name="dw", tag="dw", bufs=2)
             larger = ring.tile([P, NW], F32, name="larger", tag="larger", bufs=2)
             smaller = ring.tile([P, NW], F32, name="smaller", tag="smaller", bufs=2)
             product = ring.tile([P, NW], F32, name="product", tag="product", bufs=2)
-            nc.vector.tensor_copy(dw[:], d_win[:].indirect(pos3_t[:]))
             nc.vector.tensor_copy(aw[:], a_win[:].indirect(pos1_t[:]))
             nc.vector.tensor_tensor(larger[:], aw[:], dw[:], ALU.max)
             nc.vector.tensor_tensor(smaller[:], aw[:], dw[:], ALU.min)

@@ -79,7 +79,12 @@ def tile_list_clinic_triage_join_kernel(
 
         def round_and_deal(raw, name):
             grouped = ring.tile([P, PACK, P, PACK], BF16, name=name, tag="grouped", bufs=3, align_bytes=64)
-            nc.scalar.copy(grouped[:].rearrange("p t m i -> p m t i"), raw[:].rearrange("p i (m t) -> p m t i", t=PACK))
+            for u in range(2):
+                pair = slice(2 * u, 2 * u + 2)
+                nc.scalar.copy(
+                    grouped[:, pair].rearrange("p t m i -> p m i t"),
+                    raw[:].rearrange("p i (m t) -> p m i t", t=PACK)[:, :, :, pair],
+                )
             return grouped
 
         def quantise(flat, name):
@@ -90,8 +95,8 @@ def tile_list_clinic_triage_join_kernel(
             return codes, plane
 
         tab3_plane = zeroed_plane([P, T], "tab3_plane", nc.vector)
-        tab_plane = zeroed_plane([P, T], "tab_plane", nc.gpsimd)
         w2_plane_raw = zeroed_plane([P, H], "w2_plane_raw", nc.vector)
+        tab_plane = zeroed_plane([P, T], "tab_plane", nc.gpsimd)
         tab2_plane = zeroed_plane([P, T], "tab2_plane", nc.gpsimd)
         w4_plane = zeroed_plane([P, 2, N], "w4_plane", nc.gpsimd)
 
@@ -202,8 +207,8 @@ def tile_list_clinic_triage_join_kernel(
             w5_g = ring.tile([P, 2, N, PACK], BF16, name="w5_g", tag="w5_g", align_bytes=64)
             for a in range(2):
                 nc.scalar.copy(
-                    w5_g[:, a].rearrange("p (c k) i -> p c i k", k=4),
-                    w5_raw[a][:].rearrange("p i (c k) -> p c i k", k=4),
+                    w5_g[:, a].rearrange("p (c k) i -> p c i k", k=2),
+                    w5_raw[a][:].rearrange("p i (c k) -> p c i k", k=2),
                 )
             w5_flat = w5_g[:].rearrange("p a n i -> p (a n i)")
             for c0, c1 in ((0, 512), (512, 2 * N)):
@@ -211,11 +216,20 @@ def tile_list_clinic_triage_join_kernel(
                     out=w5_codes[:, c0:c1].bitcast(FP8X4), scales=w5_plane[:, c0:c1],
                     in_=w5_flat[:, PACK * c0 : PACK * c1])
 
-        def weave_and_quantise(b, weave):
+        def weave_and_quantise(b, weave, parts):
             z = ring.tile([P, NW, PACK], BF16, name="z", tag="grouped", bufs=3, align_bytes=64)
-            weave(z[:].rearrange("p (c i) t -> p c t i", i=4), z_rows[b][:].rearrange("p t (c i) -> p c t i", i=4))
-            return quantise(z[:].rearrange("p j t -> p (j t)"), "z%d" % b)
+            codes = keep.tile([P, NW], U32, name="z%d_codes" % b, align_bytes=64)
+            plane = keep.tile([P, NW], U8, name="z%d_plane" % b, align_bytes=64)
+            for cols in parts:
+                weave(z[:, cols].rearrange("p (c i) t -> p c t i", i=4),
+                      z_rows[b][:, :, cols].rearrange("p t (c i) -> p c t i", i=4))
+            for cols in parts:
+                nc.vector.quantize_mx(out=codes[:, cols].bitcast(FP8X4), scales=plane[:, cols],
+                                      in_=z[:, cols].rearrange("p j t -> p (j t)"))
+            return codes, plane
 
+        halves = [slice(0, NW // 2), slice(NW // 2, NW)]
+        entries = [slice(0, NW // 32), slice(NW // 32, NW // 16)]
         w5_codes = keep.tile([P, 2 * N], U32, name="w5_codes", align_bytes=64)
         w5_plane = keep.tile([P, 2 * N], U8, name="w5_plane", align_bytes=64)
         z_rows = [keep.tile([P, PACK, NW], BF16, name="z_rows%d" % b) for b in range(2)]
@@ -223,28 +237,35 @@ def tile_list_clinic_triage_join_kernel(
         for s in range(2 * PACK):
             b, t = divmod(s, PACK)
             dw = dws[s] if b == 0 else pick_d(d_rows(s))
+            last = s == 2 * PACK - 1
             a_win = a_rows(s)
+            if last:
+                z_q.append(weave_and_quantise(0, nc.scalar.copy, [slice(0, NW)]))
             b_win = b_rows(s)
             aw = ring.tile([P, NW], F32, name="aw", tag="aw", bufs=2)
             larger = ring.tile([P, NW], F32, name="larger", tag="larger", bufs=2)
             smaller = ring.tile([P, NW], F32, name="smaller", tag="smaller", bufs=2)
             product = ring.tile([P, NW], F32, name="product", tag="product", bufs=2)
-            nc.vector.tensor_copy(aw[:], a_win[:].indirect(pos1_t[:]))
-            nc.vector.tensor_tensor(larger[:], aw[:], dw[:], ALU.max)
+            for cols, part in zip(halves, entries):
+                nc.vector.tensor_copy(aw[:, cols], a_win[:].indirect(pos1_t[:, part]))
+            for cols in halves:
+                nc.vector.tensor_tensor(larger[:, cols], aw[:, cols], dw[:, cols], ALU.max)
             nc.vector.tensor_tensor(smaller[:], aw[:], dw[:], ALU.min)
-            nc.vector.tensor_tensor(product[:], b_win[:].indirect(pos2_t[:]), larger[:], ALU.mult)
-            adder = nc.vector if s == 2 * PACK - 1 else nc.gpsimd
-            adder.tensor_tensor(z_rows[b][:, t, :], product[:], smaller[:], ALU.add)
-            if s == 2:
+            if last:
+                for cols, part in zip(halves, entries):
+                    nc.vector.tensor_tensor(product[:, cols], b_win[:].indirect(pos2_t[:, part]), larger[:, cols], ALU.mult)
+                for cols in halves:
+                    nc.vector.tensor_tensor(z_rows[b][:, t, cols], product[:, cols], smaller[:, cols], ALU.add)
+            else:
+                nc.vector.tensor_tensor(product[:], b_win[:].indirect(pos2_t[:]), larger[:], ALU.mult)
+                nc.gpsimd.tensor_tensor(z_rows[b][:, t, :], product[:], smaller[:], ALU.add)
+            if s == 0:
                 prepare_w3(1)
-                prepare_w1(1, 0)
-            if s == 3:
-                prepare_w1(1, 1)
-            if s == 5:
-                z_q.append(weave_and_quantise(0, nc.scalar.copy))
+            if s in (1, 2):
+                prepare_w1(1, s - 1)
             if s == 6:
                 prepare_w5()
-        z_q.append(weave_and_quantise(1, nc.vector.tensor_copy))
+        z_q.append(weave_and_quantise(1, nc.vector.tensor_copy, halves))
 
         y4 = [psum.tile([P, NW], F32, name="y4_%d" % c, tag="acc") for c in range(3)]
         y5 = [psum.tile([P, NW], F32, name="y5_%d" % c, tag="acc") for c in range(3)]
@@ -253,11 +274,11 @@ def tile_list_clinic_triage_join_kernel(
             for c in range(3):
                 cols = slice(b * N + c * P, b * N + (c + 1) * P)
                 nc.tensor.matmul_mx(
-                    out=y5[c][:], lhsT=w5_codes[:, cols].bitcast(FP8X4), lhsT_scale=w5_plane[:, cols],
-                    rhs=z_codes[:].bitcast(FP8X4), rhs_scale=z_plane[:], start=(b == 0), stop=(b == 1))
-                nc.tensor.matmul_mx(
                     out=y4[c][:], lhsT=w4_t[:, b, 2 * c * P : 2 * (c + 1) * P].bitcast(FP4X4),
                     lhsT_scale=w4_plane[:, b, c * P : (c + 1) * P],
+                    rhs=z_codes[:].bitcast(FP8X4), rhs_scale=z_plane[:], start=(b == 0), stop=(b == 1))
+                nc.tensor.matmul_mx(
+                    out=y5[c][:], lhsT=w5_codes[:, cols].bitcast(FP8X4), lhsT_scale=w5_plane[:, cols],
                     rhs=z_codes[:].bitcast(FP8X4), rhs_scale=z_plane[:], start=(b == 0), stop=(b == 1))
         for c in range(3):
             gated = ring.tile([P, NW], F32, name="gated", tag="a", bufs=4)
@@ -265,5 +286,6 @@ def tile_list_clinic_triage_join_kernel(
             result = ring.tile([P, NW], F32, name="result", tag="b", bufs=4)
             nc.scalar.activation(gated[:], y4[c][:], ACT.Silu)
             nc.vector.tensor_tensor(weighted[:], y5[c][:], room_t[:, c, :], ALU.mult)
-            nc.vector.tensor_tensor(result[:], gated[:], weighted[:], ALU.add)
-            nc.sync.dma_start(out[c * P : (c + 1) * P, :], result[:])
+            for cols in (halves if c == 2 else [slice(0, NW)]):
+                nc.vector.tensor_tensor(result[:, cols], gated[:, cols], weighted[:, cols], ALU.add)
+                nc.sync.dma_start(out[c * P : (c + 1) * P, cols], result[:, cols])

@@ -2,8 +2,8 @@ from contextlib import ExitStack
 
 import concourse.mybir as mybir
 
-T, S, NW, K, K2, H, N = 2048, 1024, 512, 1024, 512, 1024, 384
-FLOPS = 2 * (K * H * S + 2 * K2 * H * S + 2 * H * N * NW)
+T, S, W, K, K2, H, N = 2048, 1024, 512, 1024, 512, 1024, 384
+FLOPS = 2 * (K * H * S + 2 * K2 * H * S + 2 * H * N * W)
 
 F32 = mybir.dt.float32
 BF16 = mybir.dt.bfloat16
@@ -20,6 +20,19 @@ P = 128
 PACK = 4
 K_PASS = P * PACK
 BANK = 512
+QUADRANT = 32
+SCALE_ROWS = 16
+GROUP = 16
+R_PASSES = H // K_PASS
+SLICES = H // P
+N_TILES = N // P
+MX_ALIGN = 64
+
+RAW_BUFS = 6
+ROUNDED_BUFS = 3
+WINDOW_BUFS = 4
+D_LEAD = 2
+JOIN_BUFS = 2
 
 
 def tile_list_clinic_triage_join_kernel(
@@ -34,258 +47,260 @@ def tile_list_clinic_triage_join_kernel(
         ring = ctx.enter_context(tc.tile_pool(name="ring", bufs=1))
         psum = ctx.enter_context(tc.psum_pool(name="psum", bufs=8))
 
+        r_pass = [slice(g * K_PASS, (g + 1) * K_PASS) for g in range(R_PASSES)]
+        halves = [slice(0, W // 2), slice(W // 2, W)]
+        list_halves = [slice(0, W // 2 // GROUP), slice(W // 2 // GROUP, W // GROUP)]
+
         def load_list(src, name):
             tile = lists.tile(list(src.shape), U16, name=name)
             nc.sync.dma_start(tile[:], src)
             return tile
 
-        def zeroed_plane(shape, name, engine):
-            plane = keep.tile(shape, U8, name=name, align_bytes=64)
-            flat = plane[:] if len(shape) == 2 else plane[:].rearrange("p a n -> p (a n)")
-            engine.memset(flat.bitcast(I32), 0)
+        def zeroed_plane(width, name, engine):
+            plane = keep.tile([P, width], U8, name=name, align_bytes=MX_ALIGN)
+            engine.memset(plane[:].bitcast(I32), 0)
             return plane
 
-        def load_words(words, a, name):
-            tile = keep.tile([P, T], I32, name=name, align_bytes=64)
-            nc.sync.dma_start(tile[:], words[a].rearrange("p t i -> p (t i)").bitcast(I32))
+        def load_table_words(words, g, name):
+            tile = keep.tile([P, T], I32, name=name, align_bytes=MX_ALIGN)
+            nc.sync.dma_start(tile[:], words[g].rearrange("p t i -> p (t i)").bitcast(I32))
             return tile
 
-        def load_scale_rows(plane, scales):
-            if scales.shape[0] == 2:
-                for q in range(4):
-                    nc.sync.dma_start(
-                        plane[32 * q : 32 * q + 8, :].bitcast(I32),
-                        scales[:, 4 * q : 4 * q + 4, :].bitcast(I32),
-                    )
-            else:
-                for r in range(4):
-                    nc.sync.dma_start(plane[r:P:32, :].bitcast(I32), scales[0, r:16:4, :].bitcast(I32))
+        def load_plane(plane, scales):
+            for r in range(4):
+                nc.sync.dma_start(plane[r:P:QUADRANT, :].bitcast(I32), scales[0, r:SCALE_ROWS:4, :].bitcast(I32))
 
-        def load_rows(w, a, cols, name):
-            width = cols.stop - cols.start
-            raw = ring.tile([P, PACK, width], F32, name=name, tag="raw", bufs=6)
-            nc.sync.dma_start(raw[:], w[a * K_PASS : (a + 1) * K_PASS, cols].rearrange("(p i) c -> p i c", i=PACK))
+        def load_shared_plane(plane, scales):
+            for q in range(4):
+                nc.sync.dma_start(
+                    plane[QUADRANT * q : QUADRANT * q + 8, :].bitcast(I32),
+                    scales[:, 4 * q : 4 * q + 4, :].bitcast(I32),
+                )
+
+        def load_rows(w, g, cols, name):
+            raw = ring.tile([P, PACK, cols.stop - cols.start], F32, name=name, tag="raw", bufs=RAW_BUFS)
+            nc.sync.dma_start(raw[:], w[g * K_PASS : (g + 1) * K_PASS, cols].rearrange("(p i) c -> p i c", i=PACK))
             return raw
 
-        def gather(table, offsets, dtype, name):
-            picked = keep.tile([P, S], dtype, name=name, align_bytes=64)
-            nc.vector.tensor_copy(picked[:], table[:].bitcast(dtype).indirect(offsets[:]))
+        def look_up_words(table, offsets, name):
+            picked = keep.tile([P, S], U32, name=name, align_bytes=MX_ALIGN)
+            nc.vector.tensor_copy(picked[:], table[:].bitcast(U32).indirect(offsets[:]))
             return picked
 
-        def gather_bytes(table, offsets, name):
-            picked = keep.tile([P, S], U8, name=name, align_bytes=64)
-            nc.vector.tensor_copy(picked[:], table[:].indirect(offsets[:]))
+        def look_up_plane(plane, offsets, name):
+            picked = keep.tile([P, S], U8, name=name, align_bytes=MX_ALIGN)
+            nc.vector.tensor_copy(picked[:], plane[:].indirect(offsets[:]))
             return picked
 
-        def round_and_deal(raw, name):
-            grouped = ring.tile([P, PACK, P, PACK], BF16, name=name, tag="grouped", bufs=3, align_bytes=64)
-            for u in range(2):
-                pair = slice(2 * u, 2 * u + 2)
+        def quantise_dealt(raw, name):
+            rounded = ring.tile(
+                [P, PACK, P, PACK], BF16, name=name + "_bf16", tag="rounded", bufs=ROUNDED_BUFS, align_bytes=MX_ALIGN)
+            for pair in (slice(0, 2), slice(2, 4)):
                 nc.scalar.copy(
-                    grouped[:, pair].rearrange("p t m i -> p m i t"),
+                    rounded[:, pair].rearrange("p t m i -> p m i t"),
                     raw[:].rearrange("p i (m t) -> p m i t", t=PACK)[:, :, :, pair],
                 )
-            return grouped
-
-        def quantise(flat, name):
-            width = flat.shape[1] // PACK
-            codes = keep.tile([P, width], U32, name=name + "_codes", align_bytes=64)
-            plane = keep.tile([P, width], U8, name=name + "_plane", align_bytes=64)
-            nc.vector.quantize_mx(out=codes[:].bitcast(FP8X4), scales=plane[:], in_=flat)
+            codes = keep.tile([P, K_PASS], U32, name=name + "_codes", align_bytes=MX_ALIGN)
+            plane = keep.tile([P, K_PASS], U8, name=name + "_plane", align_bytes=MX_ALIGN)
+            nc.vector.quantize_mx(
+                out=codes[:].bitcast(FP8X4), scales=plane[:], in_=rounded[:].rearrange("p t m i -> p (t m i)"))
             return codes, plane
 
-        tab3_plane = zeroed_plane([P, T], "tab3_plane", nc.vector)
-        w2_plane_raw = zeroed_plane([P, H], "w2_plane_raw", nc.vector)
-        tab_plane = zeroed_plane([P, T], "tab_plane", nc.gpsimd)
-        tab2_plane = zeroed_plane([P, T], "tab2_plane", nc.gpsimd)
-        w4_plane = zeroed_plane([P, 2, N], "w4_plane", nc.gpsimd)
+        tab3_plane = zeroed_plane(T, "tab3_plane", nc.vector)
+        w2_plane_raw = zeroed_plane(H, "w2_plane_raw", nc.vector)
+        tab_plane = zeroed_plane(T, "tab_plane", nc.gpsimd)
+        tab2_plane = zeroed_plane(T, "tab2_plane", nc.gpsimd)
+        w4_plane = zeroed_plane(R_PASSES * N, "w4_plane", nc.gpsimd)
 
-        half = [slice(b * K_PASS, (b + 1) * K_PASS) for b in range(2)]
-        w2_raw = keep.tile([P, 2 * H], U8, name="w2_raw", align_bytes=64)
+        w2_raw = keep.tile([P, 2 * H], U8, name="w2_raw", align_bytes=MX_ALIGN)
         nc.sync.dma_start(w2_raw[:].bitcast(I32), w2_words[0].bitcast(I32))
-        offs3_t = load_list(offs3, "offs3_t")
-        load_scale_rows(tab3_plane, tab3_scales)
-        tab3_t = load_words(tab3_words, 0, "tab3_t")
-        w3_raw = {0: load_rows(w3, 0, half[0], "w3_raw0")}
-        pos3_t = load_list(pos3, "pos3_t")
-        offs_t = load_list(offs, "offs_t")
-        load_scale_rows(tab_plane, tab_scales)
-        tab_t = [load_words(tab_words, a, "tab_t%d" % a) for a in range(2)]
-        offs2_t = load_list(offs2, "offs2_t")
-        load_scale_rows(tab2_plane, tab2_scales)
-        w1_raw = {(0, 0): load_rows(w1, 0, half[0], "w1_raw00")}
-        load_scale_rows(w2_plane_raw, w2_scales)
-        w1_raw[(0, 1)] = load_rows(w1, 1, half[0], "w1_raw01")
-        pos1_t = load_list(pos1, "pos1_t")
-        pos2_t = load_list(pos2, "pos2_t")
-        tab2_t = load_words(tab2_words, 0, "tab2_t")
-        w3_raw[1] = load_rows(w3, 0, half[1], "w3_raw1")
-        for a in range(2):
-            w1_raw[(1, a)] = load_rows(w1, a, half[1], "w1_raw1%d" % a)
-        w5_raw = [load_rows(w5, a, slice(0, N), "w5_raw%d" % a) for a in range(2)]
-        w4_t = keep.tile([P, 2, 2 * N], U8, name="w4_t", align_bytes=64)
-        nc.sync.dma_start(w4_t[:].bitcast(I32), w4_words.rearrange("a p n -> p a n").bitcast(I32))
+        offs3_tile = load_list(offs3, "offs3_tile")
+        load_plane(tab3_plane, tab3_scales)
+        tab3_tile = load_table_words(tab3_words, 0, "tab3_tile")
+        w3_raw = [load_rows(w3, 0, r_pass[0], "w3_raw0")]
+        offs_tile = load_list(offs, "offs_tile")
+        load_shared_plane(tab_plane, tab_scales)
+        tab_tiles = [load_table_words(tab_words, 0, "tab_tile0")]
+        offs2_tile = load_list(offs2, "offs2_tile")
+        load_plane(tab2_plane, tab2_scales)
+        pos3_tile = load_list(pos3, "pos3_tile")
+        tab_tiles.append(load_table_words(tab_words, 1, "tab_tile1"))
+        load_plane(w2_plane_raw, w2_scales)
+        w1_raw = {(0, 0): load_rows(w1, 0, r_pass[0], "w1_raw00")}
+        pos1_tile = load_list(pos1, "pos1_tile")
+        pos2_tile = load_list(pos2, "pos2_tile")
+        w1_raw[(0, 1)] = load_rows(w1, 1, r_pass[0], "w1_raw01")
+        tab2_tile = load_table_words(tab2_words, 0, "tab2_tile")
+        w3_raw.append(load_rows(w3, 0, r_pass[1], "w3_raw1"))
+        for k_pass in range(2):
+            w1_raw[(1, k_pass)] = load_rows(w1, k_pass, r_pass[1], "w1_raw1%d" % k_pass)
+        w5_raw = [load_rows(w5, g, slice(0, N), "w5_raw%d" % g) for g in range(R_PASSES)]
+        w4_tile = keep.tile([P, R_PASSES, 2 * N], U8, name="w4_tile", align_bytes=MX_ALIGN)
+        nc.sync.dma_start(w4_tile[:].bitcast(I32), w4_words.rearrange("g p n -> p g n").bitcast(I32))
         for r in range(4):
             nc.sync.dma_start(
-                w4_plane[r:P:32, :, :].bitcast(I32),
-                w4_scales[:, r:16:4, :].rearrange("a q n -> q a n").bitcast(I32),
+                w4_plane[r:P:QUADRANT, :].rearrange("q (g n) -> q g n", g=R_PASSES).bitcast(I32),
+                w4_scales[:, r:SCALE_ROWS:4, :].rearrange("g q n -> q g n").bitcast(I32),
             )
-        room_t = ring.tile([P, 3, NW], F32, name="room_t", tag="raw", bufs=6)
-        nc.sync.dma_start(room_t[:], room.rearrange("(c p) j -> p c j", p=P))
+        room_tile = ring.tile([P, N_TILES, W], F32, name="room_tile", tag="raw", bufs=RAW_BUFS)
+        nc.sync.dma_start(room_tile[:], room.rearrange("(c p) j -> p c j", p=P))
 
-        w2_t = keep.tile([P, 2 * H], U8, name="w2_t", align_bytes=64)
+        w2_tile = keep.tile([P, 2 * H], U8, name="w2_tile", align_bytes=MX_ALIGN)
         nc.vector.tensor_copy(
-            w2_t[:].bitcast(U16).rearrange("p (b t m) -> p b t m", b=2, t=PACK),
-            w2_raw[:].bitcast(U16).rearrange("p (b m t) -> p b t m", b=2, t=PACK),
+            w2_tile[:].bitcast(U16).rearrange("p (g t m) -> p g t m", g=R_PASSES, t=PACK),
+            w2_raw[:].bitcast(U16).rearrange("p (g m t) -> p g t m", g=R_PASSES, t=PACK),
         )
-        w2_plane = keep.tile([P, H], U8, name="w2_plane", align_bytes=64)
+        w2_plane = keep.tile([P, H], U8, name="w2_plane", align_bytes=MX_ALIGN)
         nc.vector.tensor_copy(
-            w2_plane[:].rearrange("p (b t m) -> p b t m", b=2, t=PACK),
-            w2_plane_raw[:].rearrange("p (b m t) -> p b t m", b=2, t=PACK),
+            w2_plane[:].rearrange("p (g t m) -> p g t m", g=R_PASSES, t=PACK),
+            w2_plane_raw[:].rearrange("p (g m t) -> p g t m", g=R_PASSES, t=PACK),
         )
 
-        def flat(grouped):
-            return grouped[:].rearrange("p t m i -> p (t m i)")
+        w1_mx, w3_mx = {}, {}
 
-        w1_q, w3_q = {}, {}
+        def prepare_w1(g, k_pass):
+            w1_mx[(g, k_pass)] = quantise_dealt(w1_raw[(g, k_pass)], "w1_%d%d" % (g, k_pass))
 
-        def prepare_w1(b, a):
-            w1_q[(b, a)] = quantise(flat(round_and_deal(w1_raw[(b, a)], "w1_g%d%d" % (b, a))), "w1_q%d%d" % (b, a))
-
-        def prepare_w3(b):
-            w3_q[b] = quantise(flat(round_and_deal(w3_raw[b], "w3_g%d" % b)), "w3_q%d" % b)
+        def prepare_w3(g):
+            w3_mx[g] = quantise_dealt(w3_raw[g], "w3_%d" % g)
 
         def first_stage(passes, tag, s):
-            window = ring.tile([P, S], F32, name="%s_win%d" % (tag, s), tag=tag, bufs=4)
-            for h in range(2):
-                cols = slice(h * BANK, (h + 1) * BANK)
+            window = ring.tile([P, S], F32, name="%s_window%d" % (tag, s), tag=tag, bufs=WINDOW_BUFS)
+            for c0 in range(0, S, BANK):
+                cols = slice(c0, c0 + BANK)
                 acc = psum.tile([P, BANK], F32, name="acc", tag="acc")
-                for i, (lhs, lhs_scale, rhs, rhs_plane, k) in enumerate(passes):
+                for i, (codes, plane, words, words_plane, first) in enumerate(passes):
                     nc.tensor.matmul_mx(
-                        out=acc[:], lhsT=lhs, lhsT_scale=lhs_scale,
-                        rhs=rhs[:, cols].bitcast(FP8X4), rhs_scale=rhs_plane[k:P, cols],
+                        out=acc[:], lhsT=codes, lhsT_scale=plane,
+                        rhs=words[:, cols].bitcast(FP8X4), rhs_scale=words_plane[first:P, cols],
                         start=(i == 0), stop=(i == len(passes) - 1),
                     )
                 nc.scalar.copy(window[:, cols], acc[:])
             return window
 
-        def a_rows(s):
-            b, t = divmod(s, PACK)
-            m = slice(t * P, (t + 1) * P)
+        def dealt_slice(mx, s):
+            codes, plane = mx
+            places = slice(s % PACK * P, (s % PACK + 1) * P)
+            return codes[:, places].bitcast(FP8X4), plane[:, places]
+
+        def a_slice(s):
             return first_stage(
-                [(w1_q[(b, a)][0][:, m].bitcast(FP8X4), w1_q[(b, a)][1][:, m], v[a], v_plane, 4 * a) for a in range(2)],
+                [dealt_slice(w1_mx[(s // PACK, k_pass)], s) + (v[k_pass], v_plane, 4 * k_pass) for k_pass in range(2)],
                 "a", s)
 
-        def d_rows(s):
-            b, t = divmod(s, PACK)
-            m = slice(t * P, (t + 1) * P)
-            return first_stage([(w3_q[b][0][:, m].bitcast(FP8X4), w3_q[b][1][:, m], v3, v3_plane, 0)], "d", s)
+        def d_slice(s):
+            return first_stage([dealt_slice(w3_mx[s // PACK], s) + (v3, v3_plane, 0)], "d", s)
 
-        def b_rows(s):
-            return first_stage(
-                [(w2_t[:, 2 * s * P : 2 * (s + 1) * P].bitcast(FP4X4), w2_plane[:, s * P : (s + 1) * P], v2, v2_plane, 0)],
-                "b", s)
+        def b_slice(s):
+            codes = w2_tile[:, 2 * s * P : 2 * (s + 1) * P].bitcast(FP4X4)
+            return first_stage([(codes, w2_plane[:, s * P : (s + 1) * P], v2, v2_plane, 0)], "b", s)
 
-        def pick_d(d_win):
-            dw = ring.tile([P, NW], F32, name="dw", tag="dw", bufs=4)
-            nc.vector.tensor_copy(dw[:], d_win[:].indirect(pos3_t[:]))
-            return dw
+        def pick_d(window):
+            picked = ring.tile([P, W], F32, name="d_picked", tag="d_picked", bufs=D_LEAD)
+            nc.vector.tensor_copy(picked[:], window[:].indirect(pos3_tile[:]))
+            return picked
 
-        v3_plane = gather_bytes(tab3_plane, offs3_t, "v3_plane")
-        v3 = gather(tab3_t, offs3_t, U32, "v3")
+        v3_plane = look_up_plane(tab3_plane, offs3_tile, "v3_plane")
+        v3 = look_up_words(tab3_tile, offs3_tile, "v3")
         prepare_w3(0)
-        d_wins = {s: d_rows(s) for s in range(PACK)}
-        v_plane = gather_bytes(tab_plane, offs_t, "v_plane")
-        v = [gather(tab_t[a], offs_t, U32, "v_%d" % a) for a in range(2)]
+        early_d_windows = [d_slice(s) for s in range(PACK)]
+        v_plane = look_up_plane(tab_plane, offs_tile, "v_plane")
+        v = [look_up_words(tab_tiles[0], offs_tile, "v_0")]
+        v2_plane = look_up_plane(tab2_plane, offs2_tile, "v2_plane")
+        v.append(look_up_words(tab_tiles[1], offs_tile, "v_1"))
         prepare_w1(0, 0)
         prepare_w1(0, 1)
-        dws = {s: pick_d(d_wins[s]) for s in range(PACK)}
-        v2_plane = gather_bytes(tab2_plane, offs2_t, "v2_plane")
-        v2 = gather(tab2_t, offs2_t, U32, "v2")
+        d_picked = [pick_d(early_d_windows[s]) for s in range(D_LEAD)]
+        v2 = look_up_words(tab2_tile, offs2_tile, "v2")
 
         def prepare_w5():
-            w5_g = ring.tile([P, 2, N, PACK], BF16, name="w5_g", tag="w5_g", align_bytes=64)
-            for a in range(2):
+            rounded = ring.tile([P, R_PASSES, N, PACK], BF16, name="w5_bf16", tag="w5_bf16", align_bytes=MX_ALIGN)
+            for g in range(R_PASSES):
                 nc.scalar.copy(
-                    w5_g[:, a].rearrange("p (c k) i -> p c i k", k=2),
-                    w5_raw[a][:].rearrange("p i (c k) -> p c i k", k=2),
+                    rounded[:, g].rearrange("p (c e) i -> p c i e", e=2),
+                    w5_raw[g][:].rearrange("p i (c e) -> p c i e", e=2),
                 )
-            w5_flat = w5_g[:].rearrange("p a n i -> p (a n i)")
-            for c0, c1 in ((0, 512), (512, 2 * N)):
+            flat = rounded[:].rearrange("p g n i -> p (g n i)")
+            for c0, c1 in ((0, 512), (512, R_PASSES * N)):
                 nc.vector.quantize_mx(
                     out=w5_codes[:, c0:c1].bitcast(FP8X4), scales=w5_plane[:, c0:c1],
-                    in_=w5_flat[:, PACK * c0 : PACK * c1])
+                    in_=flat[:, PACK * c0 : PACK * c1])
 
-        def weave_and_quantise(b, weave, parts):
-            z = ring.tile([P, NW, PACK], BF16, name="z", tag="grouped", bufs=3, align_bytes=64)
-            codes = keep.tile([P, NW], U32, name="z%d_codes" % b, align_bytes=64)
-            plane = keep.tile([P, NW], U8, name="z%d_plane" % b, align_bytes=64)
+        def weave_and_quantise(g, copy, parts):
+            woven = ring.tile([P, W, PACK], BF16, name="woven", tag="rounded", bufs=ROUNDED_BUFS, align_bytes=MX_ALIGN)
+            codes = keep.tile([P, W], U32, name="z%d_codes" % g, align_bytes=MX_ALIGN)
+            plane = keep.tile([P, W], U8, name="z%d_plane" % g, align_bytes=MX_ALIGN)
             for cols in parts:
-                weave(z[:, cols].rearrange("p (c i) t -> p c t i", i=4),
-                      z_rows[b][:, :, cols].rearrange("p t (c i) -> p c t i", i=4))
+                copy(woven[:, cols].rearrange("p (c e) t -> p c t e", e=4),
+                     z_rows[g][:, :, cols].rearrange("p t (c e) -> p c t e", e=4))
             for cols in parts:
                 nc.vector.quantize_mx(out=codes[:, cols].bitcast(FP8X4), scales=plane[:, cols],
-                                      in_=z[:, cols].rearrange("p j t -> p (j t)"))
+                                      in_=woven[:, cols].rearrange("p j t -> p (j t)"))
             return codes, plane
 
-        halves = [slice(0, NW // 2), slice(NW // 2, NW)]
-        entries = [slice(0, NW // 32), slice(NW // 32, NW // 16)]
-        w5_codes = keep.tile([P, 2 * N], U32, name="w5_codes", align_bytes=64)
-        w5_plane = keep.tile([P, 2 * N], U8, name="w5_plane", align_bytes=64)
-        z_rows = [keep.tile([P, PACK, NW], BF16, name="z_rows%d" % b) for b in range(2)]
-        z_q = []
-        for s in range(2 * PACK):
-            b, t = divmod(s, PACK)
-            dw = dws[s] if b == 0 else pick_d(d_rows(s))
-            last = s == 2 * PACK - 1
-            a_win = a_rows(s)
-            if last:
-                z_q.append(weave_and_quantise(0, nc.scalar.copy, [slice(0, NW)]))
-            b_win = b_rows(s)
-            aw = ring.tile([P, NW], F32, name="aw", tag="aw", bufs=2)
-            larger = ring.tile([P, NW], F32, name="larger", tag="larger", bufs=2)
-            smaller = ring.tile([P, NW], F32, name="smaller", tag="smaller", bufs=2)
-            product = ring.tile([P, NW], F32, name="product", tag="product", bufs=2)
-            for cols, part in zip(halves, entries):
-                nc.vector.tensor_copy(aw[:, cols], a_win[:].indirect(pos1_t[:, part]))
-            for cols in halves:
-                nc.vector.tensor_tensor(larger[:, cols], aw[:, cols], dw[:, cols], ALU.max)
-            nc.vector.tensor_tensor(smaller[:], aw[:], dw[:], ALU.min)
-            if last:
-                for cols, part in zip(halves, entries):
-                    nc.vector.tensor_tensor(product[:, cols], b_win[:].indirect(pos2_t[:, part]), larger[:, cols], ALU.mult)
-                for cols in halves:
-                    nc.vector.tensor_tensor(z_rows[b][:, t, cols], product[:, cols], smaller[:, cols], ALU.add)
-            else:
-                nc.vector.tensor_tensor(product[:], b_win[:].indirect(pos2_t[:]), larger[:], ALU.mult)
-                nc.gpsimd.tensor_tensor(z_rows[b][:, t, :], product[:], smaller[:], ALU.add)
-            if s == 0:
-                prepare_w3(1)
-            if s in (1, 2):
-                prepare_w1(1, s - 1)
-            if s == 6:
-                prepare_w5()
-        z_q.append(weave_and_quantise(1, nc.vector.tensor_copy, halves))
+        w5_codes = keep.tile([P, R_PASSES * N], U32, name="w5_codes", align_bytes=MX_ALIGN)
+        w5_plane = keep.tile([P, R_PASSES * N], U8, name="w5_plane", align_bytes=MX_ALIGN)
+        z_rows = [keep.tile([P, PACK, W], BF16, name="z_rows%d" % g) for g in range(R_PASSES)]
+        z_mx = []
+        behind_slice = {
+            0: lambda: prepare_w3(1),
+            1: lambda: prepare_w1(1, 0),
+            2: lambda: prepare_w1(1, 1),
+            SLICES - 2: prepare_w5,
+        }
 
-        y4 = [psum.tile([P, NW], F32, name="y4_%d" % c, tag="acc") for c in range(3)]
-        y5 = [psum.tile([P, NW], F32, name="y5_%d" % c, tag="acc") for c in range(3)]
-        for b in range(2):
-            z_codes, z_plane = z_q[b]
-            for c in range(3):
-                cols = slice(b * N + c * P, b * N + (c + 1) * P)
-                nc.tensor.matmul_mx(
-                    out=y4[c][:], lhsT=w4_t[:, b, 2 * c * P : 2 * (c + 1) * P].bitcast(FP4X4),
-                    lhsT_scale=w4_plane[:, b, c * P : (c + 1) * P],
-                    rhs=z_codes[:].bitcast(FP8X4), rhs_scale=z_plane[:], start=(b == 0), stop=(b == 1))
+        for s in range(SLICES):
+            g, t = divmod(s, PACK)
+            last = s == SLICES - 1
+            a_window = a_slice(s)
+            if last:
+                z_mx.append(weave_and_quantise(0, nc.scalar.copy, [slice(0, W)]))
+            b_window = b_slice(s)
+            a_picked = ring.tile([P, W], F32, name="a_picked", tag="a_picked", bufs=JOIN_BUFS)
+            larger = ring.tile([P, W], F32, name="larger", tag="larger", bufs=JOIN_BUFS)
+            smaller = ring.tile([P, W], F32, name="smaller", tag="smaller", bufs=JOIN_BUFS)
+            product = ring.tile([P, W], F32, name="product", tag="product", bufs=JOIN_BUFS)
+            for cols, entries in zip(halves, list_halves):
+                nc.vector.tensor_copy(a_picked[:, cols], a_window[:].indirect(pos1_tile[:, entries]))
+            for cols in halves:
+                nc.vector.tensor_tensor(larger[:, cols], a_picked[:, cols], d_picked[s][:, cols], ALU.max)
+            nc.vector.tensor_tensor(smaller[:], a_picked[:], d_picked[s][:], ALU.min)
+            if last:
+                for cols, entries in zip(halves, list_halves):
+                    nc.vector.tensor_tensor(
+                        product[:, cols], b_window[:].indirect(pos2_tile[:, entries]), larger[:, cols], ALU.mult)
+                for cols in halves:
+                    nc.vector.tensor_tensor(z_rows[g][:, t, cols], product[:, cols], smaller[:, cols], ALU.add)
+            else:
+                nc.vector.tensor_tensor(product[:], b_window[:].indirect(pos2_tile[:]), larger[:], ALU.mult)
+                nc.gpsimd.tensor_tensor(z_rows[g][:, t, :], product[:], smaller[:], ALU.add)
+            ahead = s + D_LEAD
+            if ahead < SLICES:
+                d_picked.append(pick_d(early_d_windows[ahead] if ahead < PACK else d_slice(ahead)))
+            if s in behind_slice:
+                behind_slice[s]()
+        z_mx.append(weave_and_quantise(1, nc.vector.tensor_copy, halves))
+
+        y4 = [psum.tile([P, W], F32, name="y4_%d" % c, tag="acc") for c in range(N_TILES)]
+        y5 = [psum.tile([P, W], F32, name="y5_%d" % c, tag="acc") for c in range(N_TILES)]
+        for g in range(R_PASSES):
+            z_codes, z_plane = z_mx[g]
+            for c in range(N_TILES):
+                cols = slice(g * N + c * P, g * N + (c + 1) * P)
                 nc.tensor.matmul_mx(
                     out=y5[c][:], lhsT=w5_codes[:, cols].bitcast(FP8X4), lhsT_scale=w5_plane[:, cols],
-                    rhs=z_codes[:].bitcast(FP8X4), rhs_scale=z_plane[:], start=(b == 0), stop=(b == 1))
-        for c in range(3):
-            gated = ring.tile([P, NW], F32, name="gated", tag="a", bufs=4)
-            weighted = ring.tile([P, NW], F32, name="weighted", tag="d", bufs=4)
-            result = ring.tile([P, NW], F32, name="result", tag="b", bufs=4)
+                    rhs=z_codes[:].bitcast(FP8X4), rhs_scale=z_plane[:], start=(g == 0), stop=(g == R_PASSES - 1))
+                nc.tensor.matmul_mx(
+                    out=y4[c][:], lhsT=w4_tile[:, g, 2 * c * P : 2 * (c + 1) * P].bitcast(FP4X4),
+                    lhsT_scale=w4_plane[:, cols],
+                    rhs=z_codes[:].bitcast(FP8X4), rhs_scale=z_plane[:], start=(g == 0), stop=(g == R_PASSES - 1))
+
+        for c in range(N_TILES):
+            gated = ring.tile([P, W], F32, name="gated", tag="a", bufs=WINDOW_BUFS)
+            weighted = ring.tile([P, W], F32, name="weighted", tag="d", bufs=WINDOW_BUFS)
+            result = ring.tile([P, W], F32, name="result", tag="b", bufs=WINDOW_BUFS)
             nc.scalar.activation(gated[:], y4[c][:], ACT.Silu)
-            nc.vector.tensor_tensor(weighted[:], y5[c][:], room_t[:, c, :], ALU.mult)
-            for cols in (halves if c == 2 else [slice(0, NW)]):
+            nc.vector.tensor_tensor(weighted[:], y5[c][:], room_tile[:, c, :], ALU.mult)
+            for cols in (halves if c == N_TILES - 1 else [slice(0, W)]):
                 nc.vector.tensor_tensor(result[:, cols], gated[:, cols], weighted[:, cols], ALU.add)
                 nc.sync.dma_start(out[c * P : (c + 1) * P, cols], result[:, cols])

from contextlib import ExitStack

import concourse.mybir as mybir

T, S, W, K, K2, H, N = 2048, 1024, 512, 1024, 512, 1024, 384
FLOPS = 2 * (K * H * S + 2 * K2 * H * S + 2 * H * N * W)

F32 = mybir.dt.float32
BF16 = mybir.dt.bfloat16
I32 = mybir.dt.int32
U32 = mybir.dt.uint32
U16 = mybir.dt.uint16
U8 = mybir.dt.uint8
FP8X4 = mybir.dt.float8_e4m3fn_x4
FP4X4 = mybir.dt.float4_e2m1fn_x4
ALU = mybir.AluOpType
ACT = mybir.ActivationFunctionType

P = 128
PACK = 4
K_PASS = P * PACK
BANK = 512
QUADRANT = 32
SCALE_ROWS = 16
GROUP = 16
R_PASSES = H // K_PASS
SLICES = H // P
N_TILES = N // P
MX_ALIGN = 64

RAW_BUFS = 6
ROUNDED_BUFS = 3
WINDOW_BUFS = 4
D_LEAD = 2
JOIN_BUFS = 2


def tile_list_clinic_triage_join_kernel(
    tc, tab_words, tab_scales, tab2_words, tab2_scales, tab3_words, tab3_scales,
    offs, offs2, offs3, pos1, pos2, pos3,
    w1, w2_words, w2_scales, w3, w4_words, w4_scales, w5, room, out,
):
    nc = tc.nc
    with ExitStack() as ctx:
        lists = ctx.enter_context(tc.tile_pool(name="lists", bufs=1))
        keep = ctx.enter_context(tc.tile_pool(name="keep", bufs=1))
        ring = ctx.enter_context(tc.tile_pool(name="ring", bufs=1))
        psum = ctx.enter_context(tc.psum_pool(name="psum", bufs=8))

        r_pass = [slice(g * K_PASS, (g + 1) * K_PASS) for g in range(R_PASSES)]
        halves = [slice(0, W // 2), slice(W // 2, W)]
        list_halves = [slice(0, W // 2 // GROUP), slice(W // 2 // GROUP, W // GROUP)]

        def load_list(src, name):
            tile = lists.tile(list(src.shape), U16, name=name)
            nc.sync.dma_start(tile[:], src)
            return tile

        def zeroed_plane(width, name, engine):
            plane = keep.tile([P, width], U8, name=name, align_bytes=MX_ALIGN)
            engine.memset(plane[:].bitcast(I32), 0)
            return plane

        def load_table_words(words, g, name):
            tile = keep.tile([P, T], I32, name=name, align_bytes=MX_ALIGN)
            nc.sync.dma_start(tile[:], words[g].rearrange("p t i -> p (t i)").bitcast(I32))
            return tile

        def load_plane(plane, scales):
            for r in range(4):
                nc.sync.dma_start(plane[r:P:QUADRANT, :].bitcast(I32), scales[0, r:SCALE_ROWS:4, :].bitcast(I32))

        def load_shared_plane(plane, scales):
            for q in range(4):
                nc.sync.dma_start(
                    plane[QUADRANT * q : QUADRANT * q + 8, :].bitcast(I32),
                    scales[:, 4 * q : 4 * q + 4, :].bitcast(I32),
                )

        def load_rows(w, g, cols, name):
            raw = ring.tile([P, PACK, cols.stop - cols.start], F32, name=name, tag="raw", bufs=RAW_BUFS)
            nc.sync.dma_start(raw[:], w[g * K_PASS : (g + 1) * K_PASS, cols].rearrange("(p i) c -> p i c", i=PACK))
            return raw

        def look_up_words(table, offsets, name):
            picked = keep.tile([P, S], U32, name=name, align_bytes=MX_ALIGN)
            nc.vector.tensor_copy(picked[:], table[:].bitcast(U32).indirect(offsets[:]))
            return picked

        def look_up_plane(plane, offsets, name):
            picked = keep.tile([P, S], U8, name=name, align_bytes=MX_ALIGN)
            nc.vector.tensor_copy(picked[:], plane[:].indirect(offsets[:]))
            return picked

        def quantise_dealt(raw, name):
            rounded = ring.tile(
                [P, PACK, P, PACK], BF16, name=name + "_bf16", tag="rounded", bufs=ROUNDED_BUFS, align_bytes=MX_ALIGN)
            for pair in (slice(0, 2), slice(2, 4)):
                nc.scalar.copy(
                    rounded[:, pair].rearrange("p t m i -> p m i t"),
                    raw[:].rearrange("p i (m t) -> p m i t", t=PACK)[:, :, :, pair],
                )
            codes = keep.tile([P, K_PASS], U32, name=name + "_codes", align_bytes=MX_ALIGN)
            plane = keep.tile([P, K_PASS], U8, name=name + "_plane", align_bytes=MX_ALIGN)
            nc.vector.quantize_mx(
                out=codes[:].bitcast(FP8X4), scales=plane[:], in_=rounded[:].rearrange("p t m i -> p (t m i)"))
            return codes, plane

        tab3_plane = zeroed_plane(T, "tab3_plane", nc.vector)
        w2_plane_raw = zeroed_plane(H, "w2_plane_raw", nc.vector)
        tab_plane = zeroed_plane(T, "tab_plane", nc.gpsimd)
        tab2_plane = zeroed_plane(T, "tab2_plane", nc.gpsimd)
        w4_plane = zeroed_plane(R_PASSES * N, "w4_plane", nc.gpsimd)

        w2_raw = keep.tile([P, 2 * H], U8, name="w2_raw", align_bytes=MX_ALIGN)
        nc.sync.dma_start(w2_raw[:].bitcast(I32), w2_words[0].bitcast(I32))
        offs3_tile = load_list(offs3, "offs3_tile")
        load_plane(tab3_plane, tab3_scales)
        tab3_tile = load_table_words(tab3_words, 0, "tab3_tile")
        w3_raw = [load_rows(w3, 0, r_pass[0], "w3_raw0")]
        offs_tile = load_list(offs, "offs_tile")
        load_shared_plane(tab_plane, tab_scales)
        tab_tiles = [load_table_words(tab_words, 0, "tab_tile0")]
        offs2_tile = load_list(offs2, "offs2_tile")
        load_plane(tab2_plane, tab2_scales)
        pos3_tile = load_list(pos3, "pos3_tile")
        tab_tiles.append(load_table_words(tab_words, 1, "tab_tile1"))
        load_plane(w2_plane_raw, w2_scales)
        w1_raw = {(0, 0): load_rows(w1, 0, r_pass[0], "w1_raw00")}
        pos1_tile = load_list(pos1, "pos1_tile")
        pos2_tile = load_list(pos2, "pos2_tile")
        w1_raw[(0, 1)] = load_rows(w1, 1, r_pass[0], "w1_raw01")
        tab2_tile = load_table_words(tab2_words, 0, "tab2_tile")
        w3_raw.append(load_rows(w3, 0, r_pass[1], "w3_raw1"))
        for k_pass in range(2):
            w1_raw[(1, k_pass)] = load_rows(w1, k_pass, r_pass[1], "w1_raw1%d" % k_pass)
        w5_raw = [load_rows(w5, g, slice(0, N), "w5_raw%d" % g) for g in range(R_PASSES)]
        w4_tile = keep.tile([P, R_PASSES, 2 * N], U8, name="w4_tile", align_bytes=MX_ALIGN)
        nc.sync.dma_start(w4_tile[:].bitcast(I32), w4_words.rearrange("g p n -> p g n").bitcast(I32))
        for r in range(4):
            nc.sync.dma_start(
                w4_plane[r:P:QUADRANT, :].rearrange("q (g n) -> q g n", g=R_PASSES).bitcast(I32),
                w4_scales[:, r:SCALE_ROWS:4, :].rearrange("g q n -> q g n").bitcast(I32),
            )
        room_tile = ring.tile([P, N_TILES, W], F32, name="room_tile", tag="raw", bufs=RAW_BUFS)
        nc.sync.dma_start(room_tile[:], room.rearrange("(c p) j -> p c j", p=P))

        w2_tile = keep.tile([P, 2 * H], U8, name="w2_tile", align_bytes=MX_ALIGN)
        nc.vector.tensor_copy(
            w2_tile[:].bitcast(U16).rearrange("p (g t m) -> p g t m", g=R_PASSES, t=PACK),
            w2_raw[:].bitcast(U16).rearrange("p (g m t) -> p g t m", g=R_PASSES, t=PACK),
        )
        w2_plane = keep.tile([P, H], U8, name="w2_plane", align_bytes=MX_ALIGN)
        nc.vector.tensor_copy(
            w2_plane[:].rearrange("p (g t m) -> p g t m", g=R_PASSES, t=PACK),
            w2_plane_raw[:].rearrange("p (g m t) -> p g t m", g=R_PASSES, t=PACK),
        )

        w1_mx, w3_mx = {}, {}

        def prepare_w1(g, k_pass):
            w1_mx[(g, k_pass)] = quantise_dealt(w1_raw[(g, k_pass)], "w1_%d%d" % (g, k_pass))

        def prepare_w3(g):
            w3_mx[g] = quantise_dealt(w3_raw[g], "w3_%d" % g)

        def first_stage(passes, tag, s):
            window = ring.tile([P, S], F32, name="%s_window%d" % (tag, s), tag=tag, bufs=WINDOW_BUFS)
            for c0 in range(0, S, BANK):
                cols = slice(c0, c0 + BANK)
                acc = psum.tile([P, BANK], F32, name="acc", tag="acc")
                for i, (codes, plane, words, words_plane, first) in enumerate(passes):
                    nc.tensor.matmul_mx(
                        out=acc[:], lhsT=codes, lhsT_scale=plane,
                        rhs=words[:, cols].bitcast(FP8X4), rhs_scale=words_plane[first:P, cols],
                        start=(i == 0), stop=(i == len(passes) - 1),
                    )
                nc.scalar.copy(window[:, cols], acc[:])
            return window

        def dealt_slice(mx, s):
            codes, plane = mx
            places = slice(s % PACK * P, (s % PACK + 1) * P)
            return codes[:, places].bitcast(FP8X4), plane[:, places]

        def a_slice(s):
            return first_stage(
                [dealt_slice(w1_mx[(s // PACK, k_pass)], s) + (v[k_pass], v_plane, 4 * k_pass) for k_pass in range(2)],
                "a", s)

        def d_slice(s):
            return first_stage([dealt_slice(w3_mx[s // PACK], s) + (v3, v3_plane, 0)], "d", s)

        def b_slice(s):
            codes = w2_tile[:, 2 * s * P : 2 * (s + 1) * P].bitcast(FP4X4)
            return first_stage([(codes, w2_plane[:, s * P : (s + 1) * P], v2, v2_plane, 0)], "b", s)

        def pick_d(window):
            picked = ring.tile([P, W], F32, name="d_picked", tag="d_picked", bufs=D_LEAD)
            nc.vector.tensor_copy(picked[:], window[:].indirect(pos3_tile[:]))
            return picked

        v3_plane = look_up_plane(tab3_plane, offs3_tile, "v3_plane")
        v3 = look_up_words(tab3_tile, offs3_tile, "v3")
        prepare_w3(0)
        early_d_windows = [d_slice(s) for s in range(PACK)]
        v_plane = look_up_plane(tab_plane, offs_tile, "v_plane")
        v = [look_up_words(tab_tiles[0], offs_tile, "v_0")]
        v2_plane = look_up_plane(tab2_plane, offs2_tile, "v2_plane")
        v.append(look_up_words(tab_tiles[1], offs_tile, "v_1"))
        prepare_w1(0, 0)
        prepare_w1(0, 1)
        d_picked = [pick_d(early_d_windows[s]) for s in range(D_LEAD)]
        v2 = look_up_words(tab2_tile, offs2_tile, "v2")

        def prepare_w5():
            rounded = ring.tile([P, R_PASSES, N, PACK], BF16, name="w5_bf16", tag="w5_bf16", align_bytes=MX_ALIGN)
            for g in range(R_PASSES):
                nc.scalar.copy(
                    rounded[:, g].rearrange("p (c e) i -> p c i e", e=2),
                    w5_raw[g][:].rearrange("p i (c e) -> p c i e", e=2),
                )
            flat = rounded[:].rearrange("p g n i -> p (g n i)")
            for c0, c1 in ((0, 512), (512, R_PASSES * N)):
                nc.vector.quantize_mx(
                    out=w5_codes[:, c0:c1].bitcast(FP8X4), scales=w5_plane[:, c0:c1],
                    in_=flat[:, PACK * c0 : PACK * c1])

        def weave_and_quantise(g, copy, parts):
            woven = ring.tile([P, W, PACK], BF16, name="woven", tag="rounded", bufs=ROUNDED_BUFS, align_bytes=MX_ALIGN)
            codes = keep.tile([P, W], U32, name="z%d_codes" % g, align_bytes=MX_ALIGN)
            plane = keep.tile([P, W], U8, name="z%d_plane" % g, align_bytes=MX_ALIGN)
            for cols in parts:
                copy(woven[:, cols].rearrange("p (c e) t -> p c t e", e=4),
                     z_rows[g][:, :, cols].rearrange("p t (c e) -> p c t e", e=4))
            for cols in parts:
                nc.vector.quantize_mx(out=codes[:, cols].bitcast(FP8X4), scales=plane[:, cols],
                                      in_=woven[:, cols].rearrange("p j t -> p (j t)"))
            return codes, plane

        w5_codes = keep.tile([P, R_PASSES * N], U32, name="w5_codes", align_bytes=MX_ALIGN)
        w5_plane = keep.tile([P, R_PASSES * N], U8, name="w5_plane", align_bytes=MX_ALIGN)
        z_rows = [keep.tile([P, PACK, W], BF16, name="z_rows%d" % g) for g in range(R_PASSES)]
        z_mx = []
        behind_slice = {
            0: lambda: prepare_w3(1),
            1: lambda: prepare_w1(1, 0),
            2: lambda: prepare_w1(1, 1),
            SLICES - 2: prepare_w5,
        }

        for s in range(SLICES):
            g, t = divmod(s, PACK)
            last = s == SLICES - 1
            a_window = a_slice(s)
            if last:
                z_mx.append(weave_and_quantise(0, nc.scalar.copy, [slice(0, W)]))
            b_window = b_slice(s)
            a_picked = ring.tile([P, W], F32, name="a_picked", tag="a_picked", bufs=JOIN_BUFS)
            larger = ring.tile([P, W], F32, name="larger", tag="larger", bufs=JOIN_BUFS)
            smaller = ring.tile([P, W], F32, name="smaller", tag="smaller", bufs=JOIN_BUFS)
            product = ring.tile([P, W], F32, name="product", tag="product", bufs=JOIN_BUFS)
            for cols, entries in zip(halves, list_halves):
                nc.vector.tensor_copy(a_picked[:, cols], a_window[:].indirect(pos1_tile[:, entries]))
            for cols in halves:
                nc.vector.tensor_tensor(larger[:, cols], a_picked[:, cols], d_picked[s][:, cols], ALU.max)
            nc.vector.tensor_tensor(smaller[:], a_picked[:], d_picked[s][:], ALU.min)
            if last:
                for cols, entries in zip(halves, list_halves):
                    nc.vector.tensor_tensor(
                        product[:, cols], b_window[:].indirect(pos2_tile[:, entries]), larger[:, cols], ALU.mult)
                for cols in halves:
                    nc.vector.tensor_tensor(z_rows[g][:, t, cols], product[:, cols], smaller[:, cols], ALU.add)
            else:
                nc.vector.tensor_tensor(product[:], b_window[:].indirect(pos2_tile[:]), larger[:], ALU.mult)
                nc.gpsimd.tensor_tensor(z_rows[g][:, t, :], product[:], smaller[:], ALU.add)
            ahead = s + D_LEAD
            if ahead < SLICES:
                d_picked.append(pick_d(early_d_windows[ahead] if ahead < PACK else d_slice(ahead)))
            if s in behind_slice:
                behind_slice[s]()
        z_mx.append(weave_and_quantise(1, nc.vector.tensor_copy, halves))

        y4 = [psum.tile([P, W], F32, name="y4_%d" % c, tag="acc") for c in range(N_TILES)]
        y5 = [psum.tile([P, W], F32, name="y5_%d" % c, tag="acc") for c in range(N_TILES)]
        for g in range(R_PASSES):
            z_codes, z_plane = z_mx[g]
            for c in range(N_TILES):
                cols = slice(g * N + c * P, g * N + (c + 1) * P)
                nc.tensor.matmul_mx(
                    out=y5[c][:], lhsT=w5_codes[:, cols].bitcast(FP8X4), lhsT_scale=w5_plane[:, cols],
                    rhs=z_codes[:].bitcast(FP8X4), rhs_scale=z_plane[:], start=(g == 0), stop=(g == R_PASSES - 1))
                nc.tensor.matmul_mx(
                    out=y4[c][:], lhsT=w4_tile[:, g, 2 * c * P : 2 * (c + 1) * P].bitcast(FP4X4),
                    lhsT_scale=w4_plane[:, cols],
                    rhs=z_codes[:].bitcast(FP8X4), rhs_scale=z_plane[:], start=(g == 0), stop=(g == R_PASSES - 1))

        for c in range(N_TILES):
            gated = ring.tile([P, W], F32, name="gated", tag="a", bufs=WINDOW_BUFS)
            weighted = ring.tile([P, W], F32, name="weighted", tag="d", bufs=WINDOW_BUFS)
            result = ring.tile([P, W], F32, name="result", tag="b", bufs=WINDOW_BUFS)
            nc.scalar.activation(gated[:], y4[c][:], ACT.Silu)
            nc.vector.tensor_tensor(weighted[:], y5[c][:], room_tile[:, c, :], ALU.mult)
            for cols in (halves if c == N_TILES - 1 else [slice(0, W)]):
                nc.vector.tensor_tensor(result[:, cols], gated[:, cols], weighted[:, cols], ALU.add)
                nc.sync.dma_start(out[c * P : (c + 1) * P, cols], result[:, cols])
